import numpy as np, ml_dtypes
CORES = [35,38,43,46]
N = 4
import mx_ref
BF = ml_dtypes.bfloat16
def gcols(t, e):
    v = np.concatenate([t.reshape(8, 16, -1, 4), np.zeros((8, 16, 1, 4), BF)], axis=2)
    return np.ascontiguousarray(np.stack([v[g][:, e[g]] for g in range(8)])).reshape(128, -1)
def tile(rs):
    return np.stack(rs, axis=2).reshape(128, -1).astype(BF)
def cut(t, i, w=512):
    return t[:, w * i:w * i + w]
def pick(q, e):
    c = np.concatenate([q[0].reshape(128, -1, 4), np.zeros((128, 1, 4), np.uint8)], axis=1); s = np.concatenate([q[1], np.ones((16, 1), np.uint8)], axis=1)
    return (np.ascontiguousarray(c[:, e].reshape(128, -1)), np.ascontiguousarray(s[:, e]))
def join(*qs):
    return (np.concatenate([q[0] for q in qs], axis=1), np.concatenate([q[1] for q in qs], axis=1))
def put(q, e, v):
    c, s = q[0].reshape(128, -1, 4).copy(), q[1].copy(); c[:, e] = v[0].reshape(128, -1, 4); s[:, e] = v[1]
    return (c.reshape(128, -1), s)
def pk(c, s):
    return (np.ascontiguousarray(c), mx_ref.live(s))
def emit(q):
    return q[0], q[1]
def packed(v, rng):
    q = [mx_ref.quantize(np.ascontiguousarray(v[r])) for r in range(N)]
    return np.stack([a for a, b in q]), np.stack([mx_ref.plane(b, rng) for a, b in q])
def values_of_codes():
    e, c = np.zeros((128, 128, 4), np.float32), np.zeros((128, 2, 4), np.uint8)
    e[np.arange(128), np.arange(128), 0] = 1
    c[:127, :, 0] = np.arange(256).reshape(2, 128).T[:127]
    return mx_ref.matmul(mx_ref.quantize(e.reshape(128, 512).astype(BF)), (c.reshape(128, 8), np.full((16, 2), 127, np.uint8))).T.reshape(-1).astype(np.float64)
CODE_VALUE, SCALE_VALUE = values_of_codes(), 2.0 ** (np.arange(256) - 127.0)
def decode(q):
    return (CODE_VALUE[q[0]].reshape(16, 8, -1, 4) * SCALE_VALUE[q[1]][:, None, :, None] + 0.0).reshape(128, -1).astype(np.float32)
def f(rng, *shape):
    return mx_ref.flush((rng.standard_normal(shape, dtype=np.float32) * np.exp2(rng.integers(-2, 3, shape[:-1] + (1,)))).astype(BF))
def wide(rng, *shape, cols=0):
    v = rng.standard_normal(shape, dtype=np.float32) * np.exp2(rng.integers(-12, 13, shape)).astype(np.float32)
    if cols: v *= np.repeat(np.exp2(rng.integers(-cols, cols + 1, shape[:-2] + (1, shape[-1] // 4))) * (rng.random(shape[:-2] + (1, shape[-1] // 4)) > 0.0625), 4, axis=-1).astype(np.float32)
    return mx_ref.flush(v.astype(BF))
T, C, M = 288, 80, 2
def big(v):
    v = v.astype(np.float32)
    v[np.abs(v) < np.float32(2.0 ** -20)] = 0
    return v.astype(BF)
def numbers_of(rng):
    return {"x": big(f(rng, N, 128, 4 * T)), "u": np.array(f(rng, N, 128, 512)), "v": np.array(f(rng, N, 128, 512))}
def weights(rng, k):
    d = {}
    for n, s in (("a", k), ("c", 1.0)):
        a = mx_ref.flush((f(rng, N, 128, 256 * M).astype(np.float32) * np.float32(s)).astype(BF)).reshape(N, 8, 16, 4 * M, 16, 4)
        w = np.zeros((N, 8, 16, 4 * M, 8, 16, 4), BF)
        for g in range(8): w[:, g, :, :, g] = a[:, g]
        d[n + "c"], d[n + "p"] = packed(w.reshape(N, 128, 2048 * M), rng)
    return d
def signs(rng):
    return np.stack([rng.permutation(8) % 2 * 2.0 - 1.0 for r in range(N)])
def setup_inputs(rng):
    return {**numbers_of(rng), **weights(rng, 1.0)}
def setup_inputs_ties(rng):
    d = numbers_of(rng)
    u = d["u"].reshape(N, 128, 8, 16, 4)
    x = d["x"].reshape(N, 128, T, 4)
    for r in range(N):
        h = rng.integers(0, 8)
        for g in range(8):
            k = np.zeros(N, int) if g == h else rng.permutation(N) % 2
            a = u[r, :, g].copy()
            u[r, :, g, :N] = a[:, k]
        x[r][:, rng.permutation(T)[:T // 16]] = 0
    return {"x": x.reshape(N, 128, 4 * T), "u": u.reshape(N, 128, 512), "v": d["v"], **weights(rng, 1.0)}
def setup_inputs_near(rng):
    d = numbers_of(rng)
    x = d["x"].astype(np.float32).reshape(N, 128, T, 4)
    kind = rng.integers(0, 15, (N, T))
    x[:, 0, :, 0] = 1
    x[:, 8::8, :, 0] = kind[:, None, :] == np.arange(15)[None, :, None]
    u = d["u"].astype(np.float32).reshape(N, 128, 8, 16, 4)
    u[:, :, :, :N] = 0
    top = rng.integers(1, N, (N, 15, 8, 1))
    k = np.arange(N)
    s = np.where(k < top, 6, np.where(k == top, 7, 6 + rng.integers(0, 2, (N, 15, 8, N))))
    u[:, 0, :, :N, 0] = signs(rng)[:, :, None]
    u[:, 8::8, :, :N, 0] = s * 2.0 ** -23
    return {"x": x.reshape(N, 128, 4 * T).astype(BF), "u": u.reshape(N, 128, 512).astype(BF), "v": d["v"], **weights(rng, 1.0)}
def setup_inputs_huge(rng):
    d = numbers_of(rng)
    m = np.arange(128) // 16 % N
    kind = rng.integers(0, N, (N, T))
    below = rng.permutation(N) < N // 2
    c = np.stack([rng.permutation(T) % 2 * 2.0 - 1.0 for r in range(N)])
    c[below] = 1
    x = np.where(m[None, :, None] == kind[:, None, :], 0.875, 0.625) * c[:, None, :]
    x = 2.0 ** 30 * x[..., None] * (0.95 + 0.1 * rng.random((N, 128, T, 4)))
    p = np.stack([np.stack([rng.permutation(N) for g in range(8)]) for r in range(N)])
    a = p[:, None] == m[None, :, None, None]
    a = np.where(below[:, None, None, None], -(1 - 0.25 * a), signs(rng)[:, None, :, None] * (0.75 + 0.25 * a))
    u = d["u"].reshape(N, 128, 8, 16, 4)
    u[:, :, :, :N] = (2.0 ** 30 * a[..., None]).astype(np.float32).astype(BF)
    return {"x": x.astype(np.float32).reshape(N, 128, 4 * T).astype(BF), "u": u.reshape(N, 128, 512), "v": d["v"], **weights(rng, 2.0 ** -8)}
def setup_inputs_caps(rng):
    d = numbers_of(rng)
    o = rng.permutation(N)
    e = np.zeros((N, 8, T), int)
    for r in range(N):
        for g in range(8):
            w = rng.permutation(N)
            w = w[w != r]
            n = np.full(N, 8)
            n[w[:3]] = [C, C + 1, 0]
            n[r] = 0
            n[r] = T - np.sum(n)
            e[r, g] = rng.permutation(np.repeat(np.arange(N), n))
    e[o[0]] = o[1]
    e[o[1]] = o[1]
    x = d["x"].astype(np.float32).reshape(N, 8, 16, T, 4)
    top = e[:, :, None, :] == np.arange(N)[None, None, :, None]
    s = np.where(top, -1.0, -1.0 - 0.5 * rng.integers(1, 3, (N, 8, N, T)))
    x[:, :, :N, :, 0] = s + 3.0 * (signs(rng) > 0)[:, :, None, None]
    u = d["u"].reshape(N, 128, 8, 16, 4)
    u[:, :, :, :N] = 0
    for g in range(8):
        for k in range(N): u[:, 16 * g + k, g, k, 0] = 2.0 ** -30
    return {"x": x.reshape(N, 128, 4 * T).astype(BF), "u": u.reshape(N, 128, 512), "v": d["v"], **weights(rng, 1.0)}
def setup_inputs_spread(rng):
    d = setup_inputs(rng)
    d["x"] = big(wide(rng, N, 128, 4 * T, cols=6))
    return d
def check_inputs(d):
    b = []
    for k in ("x", "u", "v"):
        a = np.abs(d[k].astype(np.float32))
        if not (np.isfinite(a).all() and ((a == 0) | (a >= 2.0 ** -30) & (a <= 2.0 ** 30)).all()): b.append("a value of " + k)
    g = np.arange(128) // 16
    for k in ("ac", "cc"):
        a = ((d[k] & 127) != 0).reshape(-1, 128, 4 * M, 128, 4).any(axis=(0, 2, 4))
        if (a & (g[:, None] != g[None, :])).any(): b.append("a code of " + k + " outside the blocks")
        if ((d[k] & 127) == 127).any(): b.append("a code of " + k + " is no number")
    return b
def reference(x, u, v, ac, ap, cc, cp):
    took = np.full((N, N, 8, C), -1)
    slot = np.full((N, 8, T), -1)
    for r in range(N):
        s = mx_ref.matmul(mx_ref.quantize(u[r]), mx_ref.quantize(x[r])) + np.float32(0.0)
        e = np.argmax(s.reshape(8, 16, T)[:, :N], axis=1)
        for g in range(8):
            for d in range(N):
                j = np.flatnonzero(e[g] == d)[:C]
                took[r, d, g, :len(j)] = j
                slot[r, g, j] = C * d + np.arange(len(j))
    z = []
    for d in range(N):
        a, c = pk(ac[d], ap[d]), pk(cc[d], cp[d])
        q = join(*[mx_ref.quantize(gcols(x[r], took[r, d])) for r in range(N)])
        total = None
        for i in range(M):
            h = mx_ref.quantize(tile([np.maximum(mx_ref.matmul(pick(a, 512 * i + 128 * b + np.arange(128)), q), np.float32(0.0)) * np.float32(0.0625) for b in range(4)]))
            m = [mx_ref.matmul(pick(c, 512 * i + 128 * b + np.arange(128)), h) for b in range(4)]
            total = m if i == 0 else [total[b] + m[b] for b in range(4)]
        z.append(decode(mx_ref.quantize(tile([p * np.float32(0.0625) for p in total]))).astype(BF))
    y, ol = np.zeros((N, 128, T), np.float32), np.zeros((N, 8, T), np.float32)
    oc, osc = np.zeros((N, 128, 4 * T), np.uint8), np.zeros((N, 16, T), np.uint8)
    for r in range(N):
        came = np.concatenate([cut(z[d], r, 4 * C) for d in range(N)], axis=1)
        q = mx_ref.quantize((x[r].astype(np.float32) + gcols(came, slot[r]).astype(np.float32)).astype(BF))
        y[r] = mx_ref.matmul(mx_ref.quantize(v[r]), q)
        ol[r] = slot[r]
        oc[r], osc[r] = emit(q)
    return {"y": y, "ol": ol, "oc": oc, "osc": osc}

@@ -1,0 +1,424 @@
+from concourse.bass import DstId, RemoteDMATransfer
+from concourse.mybir import dt, AluOpType, ActivationFunctionType
+
+N, TC, C = 4, 288, 80
+HW = 2 * C
+DW = 4 * C + TC
+BIG = 2048.0
+Q4, U8, BF, F32, I32, U16 = "float8_e4m3fn_x4", "uint8", "bfloat16", "float32", "int32", "uint16"
+F16 = "float16"
+
+
+def _sb(n, d):
+    return ("sbuf", [128, n], d)
+
+
+SCRATCH = {
+    "xs": _sb(4 * TC, BF), "us": _sb(512, BF), "vs": _sb(512, BF),
+    "aq": _sb(1024, Q4), "asc": _sb(1024, U8), "cq": _sb(1024, Q4), "csc": _sb(1024, U8),
+    "xq": _sb(TC, Q4), "xsc": _sb(TC, U8),
+    "uq": _sb(128, Q4), "usc": _sb(128, U8), "uq2": _sb(128, Q4), "usc2": _sb(128, U8),
+    "vq": _sb(128, Q4), "vsc": _sb(128, U8),
+    "ones": _sb(512, BF), "ebf": _sb(2048, BF), "eq": _sb(512, Q4), "esc": _sb(512, U8),
+    "ip": _sb(2, I32), "ci": _sb(6, I32), "cf": _sb(12, F32), "ul": _sb(8, I32), "uoff": _sb(8, U16),
+    "i4": _sb(C, F32), "csel": _sb(C, F32), "c152": _sb(152, F32), "vals": _sb(320, F32),
+    "pt": _sb(TC, F32), "mm": _sb(36, F32), "ww": _sb(36, F32), "ff": _sb(36, F32),
+    "fl": _sb(TC, BF), "fr": _sb(TC, BF), "cum": _sb(TC, F16), "rr": _sb(320, F16), "tt": _sb(608, F16),
+    "s152": _sb(152, F32), "loff": _sb(20, U16), "win": _sb(1216, F32), "sel": _sb(4 * C, F32), "goff": _sb(C, U16),
+    "xb": _sb(16 * C, BF),
+    "qa": _sb(HW, Q4), "sa": _sb(HW, U8), "qb": _sb(128, Q4), "sb": _sb(128, U8),
+    "la": _sb(HW, Q4), "las": _sb(HW, U8), "lb": _sb(128 + C, Q4), "lbs": _sb(128 + C, U8),
+    "hb": _sb(16 * HW, BF), "hq": _sb(4 * HW, Q4), "hs": _sb(4 * HW, U8),
+    "zb": _sb(8 * HW, BF), "zq": _sb(2 * HW, Q4), "zs": _sb(2 * HW, U8),
+    "zl": _sb(3 * C, Q4), "zls": _sb(3 * C, U8),
+    "zz": _sb(20, F32), "n1": _sb(18, F32), "n2": _sb(18, F32), "ni": _sb(18, I32), "wi": _sb(18, I32),
+    "ki": _sb(18, I32), "ov": _sb(18, F32), "w80": _sb(18, F32), "s1": _sb(18, F32), "s2": _sb(18, F32),
+    "s3": _sb(18, F32), "jr": _sb(18, F32), "jt": _sb(18, F32),
+    "hoff": _sb(18, U16), "tab": _sb(DW, F32), "olr": _sb(TC, F32),
+    "dw": _sb(4 * DW, BF), "yb": _sb(4 * TC, BF), "yq": _sb(TC, Q4), "ysc": _sb(TC, U8), "yo": _sb(TC, F32),
+    "pp": ("psum", [128, 4096], F32),
+}
+SEMAPHORES = ["arr_far", "arr_near", "home", "sent"] + ["s%d" % i for i in range(140)]
+
+OP = AluOpType
+ACT = ActivationFunctionType
+
+
+def rank_program(g, core, T, topo):
+    r = T.rank_of(core)
+    if r is None:
+        return
+    cores = list(T.cores)
+    V, S, PE, SY = g.vector, g.scalar, g.tensor, g.sync
+    queues = {"V": V, "S": S, "PE": PE, "SY": SY, "G": g}
+    toks = []
+
+    def tok():
+        t = {"sem": T.sem["s%d" % len(toks)], "n": 0, "w": []}
+        toks.append(t)
+        return t
+
+    def done(ins, t=None, k=1):
+        if t is None:
+            t = tok()
+        ins.then_inc(t["sem"], k)
+        t["n"] += k
+        return t
+
+    def wait(q, *ts):
+        for t in ts:
+            if q not in t["w"]:
+                queues[q].wait_ge(t["sem"], t["n"])
+                t["w"].append(q)
+
+    def slot_home(home, d):
+        return (d + N - 1 - home) % N
+
+    def far_of(a):
+        ds = [d for d in range(N) if topo.chip(cores[d]) != topo.chip(cores[a])]
+        return sorted(ds, key=lambda d: slot_home(a, d))
+
+    far = far_of(r)
+    near = [d for d in range(N) if d != r and d not in far][0]
+    order = far + [near, r]
+    slot = [slot_home(r, d) for d in order]
+    far_eng = topo.engines(core, cores[far[0]])
+    near_eng = [e for e in topo.engines(core, cores[near]) if e not in far_eng]
+    half = len(far_eng) // 2
+
+    def mask_of(es):
+        m = 0
+        for e in es:
+            m |= 1 << e
+        return m
+
+    far_masks = [mask_of(far_eng[:half]), mask_of(far_eng[half:])]
+    near_mask = mask_of(near_eng)
+    sent = [0]
+
+    def b8(ap):
+        return ap.bitcast(dt.uint8)
+
+    def send_far(srcs, dsts, sem):
+        trs = []
+        for i, d in enumerate(far):
+            rid, pid, _se = topo.addr(cores[d])
+            trs.append(RemoteDMATransfer(dst_ids=[DstId(rid=rid, pnc=pid)], dma_engine_mask=far_masks[i],
+                                         remote_sem=sem, src=srcs[i], dst=dsts[i]))
+        g.remote_dma_fused(trs, local_sem=T.sem.sent)
+        sent[0] += 2 * half
+
+    def send_near(src, dst, sem):
+        rid, pid, _se = topo.addr(cores[near])
+        g.remote_dma(dst, src, sem, T.sem.sent, pid, rid, near_mask)
+        sent[0] += len(near_eng)
+
+    def bank(b, n):
+        return T.pp[:, 512 * b:512 * b + n]
+
+    t_u = done(SY.dma_start(T.us[:], T.u[:]), k=16)
+    t_x = done(SY.dma_start(T.xs[:], T.x[:]), k=16)
+    t_a = done(SY.dma_start(b8(T.aq[:]), T.ac[:]), k=16)
+    done(SY.dma_start(T.asc[:], T.ap[:]), t_a, 16)
+    t_c = done(SY.dma_start(b8(T.cq[:]), T.cc[:]), k=16)
+    done(SY.dma_start(T.csc[:], T.cp[:]), t_c, 16)
+    SY.wait_ge(T.sem.arr_far, 4 * half)
+    t_v = done(SY.dma_start(T.vs[:], T.v[:]), k=16)
+
+    fl_ok = {"allow_small_or_imprecise_dtypes": True}
+    t_ip = done(g.iota(T.ip[:], [[4 * (N - 1 - r), 2]], 0, 1))
+    t_ul = done(g.iota(T.ul[:], [[16, 8]], 0, 0))
+    t_i4 = done(g.iota(T.i4[:], [[0, C // 4], [1, 4]], 0, 0, **fl_ok))
+    t_vals = done(g.iota(T.vals[:], [[64, 2], [128, 10], [4, 16]], -64, 0, **fl_ok))
+
+    t_ones = done(V.memset(T.ones[:], 1.0))
+    wait("S", t_ones)
+    t_z1 = done(S.activation(T.c152[:], T.ones[:, 0:152], ACT.Identity, scale=0.0))
+    t_z = done(S.activation(T.fl[:], T.ones[:, 0:TC], ACT.Identity, scale=0.0))
+    done(S.activation(T.win[:, 0:4 * C], T.ones[:, 0:4 * C], ACT.Identity, scale=0.0), t_z)
+
+    wait("G", t_ones)
+    t_e = tok()
+    for b in range(4):
+        done(g.affine_select(T.ebf[:, 512 * b:512 * b + 512], T.ones[:], [[1, 512]], OP.is_equal, 0.0, -b, -4), t_e)
+
+    ai, wi_, ti, hi, qi = [T.ci[:, k:k + 1] for k in range(5)]
+    acol, winit, hcol, sub1, c4, x1, nh, x2, sub2, qcol = [T.cf[:, k:k + 1] for k in range(10)]
+    wait("V", t_ip)
+    t_l1 = done(V.tensor_scalar(T.ci[:, 0:2], T.ip[:], 2, 3, OP.logical_shift_right, OP.bitwise_and))
+    done(V.tensor_scalar(ti, T.ip[:, 0:1], 3, None, OP.bitwise_and), t_l1)
+    done(V.tensor_scalar(hi, T.ip[:, 0:1], 4, 1, OP.logical_shift_right, OP.bitwise_and), t_l1)
+    wait("V", t_l1)
+    t_l2 = done(V.tensor_copy(acol, ai))
+    done(V.tensor_scalar(c4, hi, -5.0 * BIG, BIG, OP.mult, OP.add), t_l2)
+    done(V.tensor_scalar(x1, ai, -BIG, 3.0 * BIG, OP.mult, OP.add), t_l2)
+    t_l2b = done(V.tensor_scalar(winit, wi_, 0.25, None, OP.mult))
+    done(V.tensor_scalar(sub1, hi, -BIG, BIG + 1.0, OP.mult, OP.add), t_l2b)
+    wait("V", t_l2, t_ul)
+    t_uo = done(V.tensor_scalar(T.uoff[:], T.ul[:], acol, None, OP.add))
+    t_x2 = done(V.tensor_scalar(x2, hi, -64.0, x1, OP.mult, OP.add))
+    wait("V", t_i4)
+    t_cs = done(V.tensor_scalar(T.csel[:], T.i4[:], acol, -8.0 * BIG, OP.is_equal, OP.mult))
+    wait("V", t_x2)
+    t_l4 = done(V.tensor_scalar(sub2, ti, -1.0, x2, OP.mult, OP.add))
+
+    wait("S", t_z1, t_l2)
+    done(S.activation(T.c152[:, 0:152:8], T.ones[:, 0:19], ACT.Identity, scale=-4.0 * BIG), t_z)
+    done(S.activation(T.c152[:, 4:152:8], T.ones[:, 0:19], ACT.Identity, scale=c4), t_z)
+
+    wait("V", t_u)
+    t_qu = done(V.quantize_mx(T.uq[:], T.usc[:], T.us[:]))
+    wait("V", t_qu, t_uo)
+    t_pu = done(V.tensor_copy(T.uq2[:].bitcast(dt.uint32), T.uq[:].bitcast(dt.uint32).indirect(T.uoff[:])))
+    wait("S", t_qu, t_uo)
+    done(S.activation(T.usc2[:], T.usc[:].indirect(T.uoff[:]), ACT.Copy), t_pu)
+
+    wait("V", t_x)
+    t_qx = done(V.quantize_mx(T.xq[:], T.xsc[:], T.xs[:]))
+    wait("V", t_vals, t_cs)
+    t_pad = done(V.tensor_scalar(T.rr[:, 0:16], T.vals[:, 0:16], 0.25, TC + 17.0, OP.mult, OP.add))
+    done(V.tensor_scalar(T.rr[:, 304:320], T.vals[:, 0:16], 0.25, TC + 17.0, OP.mult, OP.add), t_pad)
+    done(V.tensor_scalar(T.csel[:], T.csel[:], BIG, None, OP.add), t_l4)
+
+    wait("PE", t_pu, t_qx)
+    t_p = done(PE.matmul_mx(bank(0, TC), T.uq2[:], T.usc2[:], T.xq[:], T.xsc[:], True, True))
+
+    wait("V", t_z, t_l2b, t_pad, t_l4, t_p)
+    t_pt = done(V.transpose(T.pt[:], bank(0, TC)))
+    wait("V", t_pt)
+    ev, od = T.pt[:, 0:TC:8], T.pt[:, 4:TC:8]
+    t1 = done(V.tensor_tensor(T.mm[:], ev, od, OP.max))
+    t2 = done(V.tensor_tensor(T.ww[:], ev, od, OP.is_ge))
+    wait("V", t1)
+    done(V.tensor_tensor(T.ff[:, 0:36:2], T.mm[:, 0:36:2], T.mm[:, 1:36:2], OP.is_ge), t2)
+    done(V.tensor_tensor(T.ff[:, 1:36:2], T.mm[:, 0:36:2], T.mm[:, 1:36:2], OP.is_lt), t2)
+    wait("V", t2)
+    t3 = done(V.tensor_tensor(T.fl[:, 0:TC:8], T.ff[:], T.ww[:], OP.mult))
+    done(V.tensor_tensor(T.fl[:, 4:TC:8], T.ff[:], T.ww[:], OP.is_gt), t3)
+    wait("V", t3)
+    t4 = done(V.transpose(T.fr[:], T.fl[:]))
+    wait("V", t4)
+    t5 = done(V.tensor_tensor_scan(T.cum[:], T.fr[:], T.fr[:], winit, OP.add, OP.max))
+    wait("V", t5)
+    t6 = done(V.tensor_tensor_scan(T.rr[:, 16:304], T.cum[:], T.fr[:], 0.0, OP.max, OP.mult))
+    wait("V", t6)
+    t7 = done(V.transpose(T.tt[:, 0:320], T.rr[:, 0:320]))
+    done(V.transpose(T.tt[:, 320:608], T.rr[:, 16:304]), t7)
+    wait("V", t7)
+    t8 = done(V.tensor_tensor_scan(T.s152[:], T.c152[:], T.tt[:, 0:608:4], 0.0, OP.add, OP.max))
+    wait("V", t8)
+    t9 = done(V.tensor_scalar(T.loff[:, 0:19], T.s152[:, 7:152:8], sub1, 4.0, OP.subtract, OP.mult))
+    wait("V", t9)
+    t10 = done(V.tensor_copy(T.win[:].indirect(T.loff[:, 0:19]), T.vals[:, 0:304]))
+    wait("V", t10)
+
+    def select(lo):
+        t = tok()
+        for i in (lo, lo + 1):
+            done(V.tensor_tensor_scan(T.sel[:, C * i:C * i + C], T.csel[:], T.win[:, slot[i]:4 * C:4], 0.0,
+                                      OP.add, OP.max), t)
+        wait("V", t)
+        return done(V.tensor_scalar(T.goff[:, 20 * lo:20 * lo + 40], T.sel[:, C * lo + 3:C * lo + HW:4], sub2, None,
+                                    OP.subtract))
+
+    def gather(q, dst, src, t=None):
+        if q == "V":
+            return done(V.tensor_copy(dst, src), t)
+        return done(S.activation(dst, src, ACT.Copy), t)
+
+    def bundle(q, i, t=None):
+        return gather(q, T.xb[:, 4 * C * slot[i]:4 * C * (slot[i] + 1)],
+                      T.xs[:].indirect(T.goff[:, 20 * i:20 * i + 20]), t)
+
+    t_ga = select(0)
+    wait("V", t_ga)
+    t_b01 = bundle("V", 0)
+    wait("S", t_x, t_ga)
+    bundle("S", 1, t_b01)
+    wait("V", t_b01)
+    t_q1 = done(V.quantize_mx(T.qa[:], T.sa[:], T.xb[:, 4 * C * slot[0]:4 * C * slot[0] + 4 * HW]))
+    t_gb = select(2)
+    wait("V", t_gb)
+    t_b2 = bundle("V", 2)
+    wait("S", t_gb)
+    t_b3 = bundle("S", 3)
+    wait("V", t_b2)
+    n0 = max(0, C * slot[2] + C - 128)
+    nb = C * slot[2] - n0
+    t_q2 = done(V.quantize_mx(T.qb[:], T.sb[:], T.xb[:, 4 * n0:4 * (n0 + 128)]))
+    wait("V", t_b3)
+    t_q3 = done(V.quantize_mx(T.lb[:, 0:128], T.lbs[:, 0:128], T.xb[:, 4 * (4 * C - 128):4 * 4 * C]))
+
+    at = [C * far_of(d).index(r) for d in far]
+    wait("G", t_q1)
+    send_far([b8(T.qa[:, C * i:C * i + C]) for i in range(2)], [b8(T.la[:, a:a + C]) for a in at], T.sem.arr_far)
+    send_far([T.sa[:, C * i:C * i + C] for i in range(2)], [T.las[:, a:a + C] for a in at], T.sem.arr_far)
+    wait("G", t_q2)
+    send_near(b8(T.qb[:, nb:nb + C]), b8(T.lb[:, 128:128 + C]), T.sem.arr_near)
+    send_near(T.sb[:, nb:nb + C], T.lbs[:, 128:128 + C], T.sem.arr_near)
+
+    t_jr = done(g.iota(T.jr[:], [[16, 18]], 4 * C, 0, **fl_ok))
+    n_hi = 4 * C - C * (r + 1)
+    t_tab = tok()
+    if n_hi:
+        done(g.iota(T.tab[:, 0:n_hi], [[1, n_hi]], C * (r + 1), 0, **fl_ok), t_tab)
+    done(g.iota(T.tab[:, n_hi:4 * C], [[1, 4 * C - n_hi]], 0, 0, **fl_ok), t_tab)
+    t_xw = tok()
+    for b in range(4):
+        done(S.activation(T.dw[:, DW * b + 4 * C:DW * (b + 1)], T.xs[:, b:4 * TC:4], ACT.Copy), t_xw)
+    done(S.activation(T.tab[:, 4 * C:DW], T.ones[:, 0:TC], ACT.Identity, scale=-1.0), t_tab)
+
+    h1 = done(V.tensor_scalar(T.zz[:, 0:19:2], T.s152[:, 7:80:8], sub1, 4.0, OP.subtract, OP.mult))
+    done(V.tensor_scalar(T.zz[:, 1:19:2], T.s152[:, 87:152:8], sub1, 4.0, OP.subtract, OP.mult), h1)
+    done(V.tensor_copy(hcol, hi), h1)
+    done(V.tensor_scalar(nh, hi, -1.0, 1.0, OP.mult, OP.add), h1)
+    done(V.tensor_scalar(qi, T.ip[:, 0:1], 15, None, OP.bitwise_and), h1)
+    wait("V", h1)
+    h2 = done(V.tensor_scalar(T.n1[:], T.zz[:, 1:19], nh, None, OP.mult))
+    done(V.tensor_scalar(T.n2[:], T.zz[:, 0:18], hcol, None, OP.mult), h2)
+    done(V.tensor_copy(qcol, qi), h2)
+    wait("V", h2)
+    h3 = done(V.tensor_tensor(T.ni[:], T.n1[:], T.n2[:], OP.add))
+    wait("V", h3)
+    h4 = done(V.tensor_scalar(T.wi[:], T.ni[:], 3, None, OP.bitwise_and))
+    done(V.tensor_scalar(T.ki[:], T.ni[:], 2, None, OP.logical_shift_right), h4)
+    done(V.tensor_scalar(T.ov[:], T.ni[:], 4.0 * C, BIG, OP.is_ge, OP.mult), h4)
+    wait("V", h4)
+    h5 = done(V.tensor_scalar(T.w80[:], T.wi[:], float(C), None, OP.mult))
+    done(V.tensor_tensor(T.s1[:], T.ki[:], T.ov[:], OP.add), h5)
+    wait("V", h5)
+    h6 = done(V.tensor_tensor(T.s2[:], T.s1[:], T.w80[:], OP.add))
+    wait("V", t_e)
+    t_qe = done(V.quantize_mx(T.eq[:], T.esc[:], T.ebf[:]))
+
+    def relu(q, dst, src, t):
+        if q == "V":
+            return done(V.tensor_scalar(dst, src, 0.0, 0.0625, OP.max, OP.mult), t)
+        return done(S.activation(dst, src, ACT.Relu, scale=0.0625), t)
+
+    def scaled(q, dst, src, t):
+        if q == "V":
+            return done(V.tensor_scalar(dst, src, 0.0625, None, OP.mult), t)
+        return done(S.activation(dst, src, ACT.Identity, scale=0.0625), t)
+
+    def layer(q, s, i, b0, mq, ms, start, stop):
+        ts = []
+        for b in range(4):
+            k = 512 * i + 128 * b
+            ins = PE.matmul_mx(bank(b0 + b, HW), q[:, k:k + 128], s[:, k:k + 128], mq, ms, start, stop)
+            ts.append(done(ins) if stop else None)
+        return ts
+
+    def htile(hf, i):
+        n = 2 * hf + i
+        return 4 * HW * n, T.hq[:, HW * n:HW * n + HW], T.hs[:, HW * n:HW * n + HW]
+
+    def evict(fn, buf, o, b0, ts, who, t):
+        for q, b in who:
+            wait(q, ts[b])
+            fn(q, buf[:, o + b:o + 4 * HW:4], bank(b0 + b, HW), t)
+
+    def expert(hf, mq, ms, bx, by, free_y):
+        o0, q0, s0 = htile(hf, 0)
+        o1, q1, s1 = htile(hf, 1)
+        ta0 = layer(T.aq, T.asc, 0, bx, mq, ms, True, True)
+        wait("PE", *free_y)
+        ta1 = layer(T.aq, T.asc, 1, by, mq, ms, True, True)
+        e0, e1, ez = tok(), tok(), tok()
+        evict(relu, T.hb, o0, bx, ta0, (("V", 0), ("S", 1), ("V", 2), ("S", 3)), e0)
+        wait("V", e0)
+        th0 = done(V.quantize_mx(q0, s0, T.hb[:, o0:o0 + 4 * HW]))
+        evict(relu, T.hb, o1, by, ta1, (("S", 0), ("S", 1), ("V", 2), ("S", 3)), e1)
+        wait("V", e1)
+        th1 = done(V.quantize_mx(q1, s1, T.hb[:, o1:o1 + 4 * HW]))
+        wait("PE", t_c, th0)
+        layer(T.cq, T.csc, 0, bx, q0, s0, True, False)
+        wait("PE", th1)
+        tc = layer(T.cq, T.csc, 1, bx, q1, s1, False, True)
+        oz = 4 * HW * hf
+        evict(scaled, T.zb, oz, bx, tc, (("V", 0), ("S", 1), ("V", 2), ("S", 3)), ez)
+        wait("V", ez)
+        return done(V.quantize_mx(T.zq[:, HW * hf:HW * hf + HW], T.zs[:, HW * hf:HW * hf + HW],
+                                  T.zb[:, oz:oz + 4 * HW]))
+
+    wait("PE", t_pt, t_a, t_q3)
+    PE.wait_ge(T.sem.arr_far, 4 * half)
+    t_za = expert(0, T.la[:], T.las[:], 0, 4, [])
+    PE.wait_ge(T.sem.arr_near, 2 * len(near_eng))
+    t_zb = expert(1, T.lb[:, 128 - C:128 + C], T.lbs[:, 128 - C:128 + C], 4, 0, [t_za])
+
+    hm = [C * slot_home(d, r) for d in far]
+    wait("G", t_za)
+    send_far([b8(T.zq[:, C * i:C * i + C]) for i in range(2)], [b8(T.zl[:, a:a + C]) for a in hm], T.sem.home)
+    send_far([T.zs[:, C * i:C * i + C] for i in range(2)], [T.zls[:, a:a + C] for a in hm], T.sem.home)
+    hn = C * slot_home(near, r)
+    wait("G", t_zb)
+    send_near(b8(T.zq[:, 3 * C:4 * C]), b8(T.zl[:, hn:hn + C]), T.sem.home)
+    send_near(T.zs[:, 3 * C:4 * C], T.zls[:, hn:hn + C], T.sem.home)
+
+    def decode(b0, mq, ms, n, keep, c0, ts):
+        out = []
+        for b in range(4):
+            t = done(PE.matmul_mx(bank(b0 + b, n), T.eq[:, 128 * b:128 * b + 128], T.esc[:, 128 * b:128 * b + 128],
+                                  mq, ms, True, True))
+            wait("V", t)
+            out.append(done(V.tensor_tensor(T.dw[:, DW * b + c0:DW * b + c0 + keep], bank(b0 + b, keep),
+                                            T.xb[:, 4 * c0 + b:4 * (c0 + keep):4], OP.add), ts))
+        return out
+
+    wait("V", h6, t_jr)
+    h7 = done(V.tensor_scalar(T.jt[:], T.jr[:], qcol, None, OP.add))
+    wait("V", h7)
+    h8 = done(V.tensor_tensor(T.s3[:], T.s2[:], T.jt[:], OP.min))
+    wait("V", h8)
+    t_h = done(V.tensor_copy(T.hoff[:], T.s3[:]))
+    wait("PE", t_qe, t_zb)
+    t_own = tok()
+    decode(0, T.zq[:, HW:HW + 128], T.zs[:, HW:HW + 128], 128, C, 3 * C, t_own)
+    wait("V", t_v)
+    t_qv = done(V.quantize_mx(T.vq[:], T.vsc[:], T.vs[:]))
+
+    wait("S", t_h, t_tab)
+    t_olr = done(S.activation(T.olr[:], T.tab[:].indirect(T.hoff[:]), ACT.Copy))
+    wait("SY", t_olr)
+    t_out = done(SY.dma_start(T.ol[:], T.olr[0:128:16, :]), k=16)
+
+    wait("PE", t_own, t_qv)
+    wait("V", t_h, t_own, t_xw)
+    wait("S", t_own, t_xw)
+    PE.wait_ge(T.sem.home, 4 * half + 2 * len(near_eng))
+    t_d = decode(4, T.zl[:], T.zls[:], 3 * C, 3 * C, 0, None)
+
+    runs = ((0, HW), (HW, TC))
+    who = (("S", "S", "S", "V"), ("S", "S", "V", "V"))
+    ty = [tok(), tok()]
+
+    def pick_y(q, n):
+        j0, j1 = runs[n]
+        for b in (range(4) if q == "S" else range(3, -1, -1)):
+            if who[n][b] == q:
+                wait(q, t_d[b])
+                gather(q, T.yb[:, 4 * j0 + b:4 * j1:4],
+                       T.dw[:, DW * b:DW * (b + 1)].indirect(T.hoff[:, j0 // 16:j1 // 16]), ty[n])
+
+    pick_y("S", 0)
+    pick_y("S", 1)
+    for n, (j0, j1) in enumerate(runs):
+        pick_y("V", n)
+        wait("V", ty[n])
+        tq = done(V.quantize_mx(T.yq[:, j0:j1], T.ysc[:, j0:j1], T.yb[:, 4 * j0:4 * j1]))
+        wait("PE", tq)
+        tm = done(PE.matmul_mx(bank(n, j1 - j0), T.vq[:], T.vsc[:], T.yq[:, j0:j1], T.ysc[:, j0:j1], True, True))
+        wait("S", tm)
+        te = done(S.activation(T.yo[:, j0:j1], bank(n, j1 - j0), ACT.Copy))
+        wait("S", te)
+        done(S.dma_start(T.y[:, j0:j1], T.yo[:, j0:j1]), t_out, 16)
+        wait("SY", tq)
+        done(SY.dma_start(T.oc[:, 4 * j0:4 * j1], b8(T.yq[:, j0:j1])), t_out, 16)
+    for k in range(4):
+        done(SY.dma_start(T.osc[4 * k:4 * k + 4, :], T.ysc[32 * k:32 * k + 4, :]), t_out, 16)
+
+    g.wait_ge(T.sem.sent, sent[0])
+    for t in toks:
+        if not t["w"] and t["n"]:
+            wait("SY", t)

@@ -3,10 +3,14 @@ from concourse.mybir import dt, AluOpType, ActivationFunctionType
 
 N, TC, C = 4, 288, 80
 HW = 2 * C
+PAD = 128 - C
 DW = 4 * C + TC
 BIG = 2048.0
+NL = TC // 16
 Q4, U8, BF, F32, I32, U16 = "float8_e4m3fn_x4", "uint8", "bfloat16", "float32", "int32", "uint16"
 F16 = "float16"
+RAW = (0, 2)
+SUM = (1, 3)
 
 
 def _sb(n, d):
@@ -19,26 +23,26 @@ SCRATCH = {
     "xq": _sb(TC, Q4), "xsc": _sb(TC, U8),
     "uq": _sb(128, Q4), "usc": _sb(128, U8), "uq2": _sb(128, Q4), "usc2": _sb(128, U8),
     "vq": _sb(128, Q4), "vsc": _sb(128, U8),
-    "ones": _sb(512, BF), "ebf": _sb(2048, BF), "eq": _sb(512, Q4), "esc": _sb(512, U8),
-    "ip": _sb(2, I32), "ci": _sb(6, I32), "cf": _sb(12, F32), "ul": _sb(8, I32), "uoff": _sb(8, U16),
-    "i4": _sb(C, F32), "csel": _sb(C, F32), "c152": _sb(152, F32), "vals": _sb(320, F32),
+    "ones": _sb(320, BF), "ebf": _sb(2048, BF), "eq": _sb(512, Q4), "esc": _sb(512, U8),
+    "ip": _sb(3, I32), "ci": _sb(5, I32), "cf": _sb(5, F32), "cs": _sb(5, F32), "ul": _sb(8, I32),
+    "uoff": _sb(8, U16), "gl": _sb(2, U16),
+    "csel": _sb(C, F32), "c152": _sb(152, F32), "vals": _sb(TC, F32),
     "pt": _sb(TC, F32), "mm": _sb(36, F32), "ww": _sb(36, F32), "ff": _sb(36, F32),
     "fl": _sb(TC, BF), "fr": _sb(TC, BF), "cum": _sb(TC, F16), "rr": _sb(320, F16), "tt": _sb(608, F16),
-    "s152": _sb(152, F32), "loff": _sb(20, U16), "win": _sb(1216, F32), "sel": _sb(4 * C, F32), "goff": _sb(C, U16),
-    "xb": _sb(16 * C, BF),
-    "qa": _sb(HW, Q4), "sa": _sb(HW, U8), "qb": _sb(128, Q4), "sb": _sb(128, U8),
-    "la": _sb(HW, Q4), "las": _sb(HW, U8), "lb": _sb(128 + C, Q4), "lbs": _sb(128 + C, U8),
-    "hb": _sb(16 * HW, BF), "hq": _sb(4 * HW, Q4), "hs": _sb(4 * HW, U8),
-    "zb": _sb(8 * HW, BF), "zq": _sb(2 * HW, Q4), "zs": _sb(2 * HW, U8),
+    "s152": _sb(152, F32), "loff": _sb(32, U16), "win": _sb(4 * TC, F32), "sel": _sb(4 * C, F32),
+    "goff": _sb(C, U16), "xb": _sb(16 * C, BF),
+    "qa": _sb(HW, Q4), "sa": _sb(HW, U8), "qb": _sb(3 * C, Q4), "sb": _sb(3 * C, U8),
+    "la": _sb(HW, Q4), "las": _sb(HW, U8),
+    "hf": _sb(12 * HW, BF), "hn": _sb(4 * (PAD + 6 * C), BF),
+    "hq": _sb(2 * HW + 4 * 128, Q4), "hs": _sb(2 * HW + 4 * 128, U8),
+    "zq": _sb(HW + 2 * 128, Q4), "zs": _sb(HW + 2 * 128, U8),
     "zl": _sb(3 * C, Q4), "zls": _sb(3 * C, U8),
-    "zz": _sb(20, F32), "n1": _sb(18, F32), "n2": _sb(18, F32), "ni": _sb(18, I32), "wi": _sb(18, I32),
-    "ki": _sb(18, I32), "ov": _sb(18, F32), "w80": _sb(18, F32), "s1": _sb(18, F32), "s2": _sb(18, F32),
-    "s3": _sb(18, F32), "jr": _sb(18, F32), "jt": _sb(18, F32),
-    "hoff": _sb(18, U16), "tab": _sb(DW, F32), "olr": _sb(TC, F32),
+    "jr": _sb(32, F32), "d0": _sb(64, F32), "d1": _sb(64, F32), "d2": _sb(64, F32),
+    "hoff": _sb(NL, U16), "tab": _sb(DW, F32), "olr": _sb(TC, F32),
     "dw": _sb(4 * DW, BF), "yb": _sb(4 * TC, BF), "yq": _sb(TC, Q4), "ysc": _sb(TC, U8), "yo": _sb(TC, F32),
     "pp": ("psum", [128, 4096], F32),
 }
-SEMAPHORES = ["arr_far", "arr_near", "home", "sent"] + ["s%d" % i for i in range(140)]
+SEMAPHORES = ["arr_far", "arr_near", "home_far", "home_near", "sent"] + ["s%d" % i for i in range(145)]
 
 OP = AluOpType
 ACT = ActivationFunctionType
@@ -54,7 +58,7 @@ def rank_program(g, core, T, topo):
     toks = []
 
     def tok():
-        t = {"sem": T.sem["s%d" % len(toks)], "n": 0, "w": []}
+        t = {"sem": T.sem["s%d" % len(toks)], "n": 0, "w": {}}
         toks.append(t)
         return t
 
@@ -67,21 +71,22 @@ def rank_program(g, core, T, topo):
 
     def wait(q, *ts):
         for t in ts:
-            if q not in t["w"]:
+            if t["w"].get(q, 0) < t["n"]:
                 queues[q].wait_ge(t["sem"], t["n"])
-                t["w"].append(q)
+                t["w"][q] = t["n"]
 
-    def slot_home(home, d):
-        return (d + N - 1 - home) % N
+    def near_of(a):
+        return [d for d in range(N) if d != a and topo.chip(cores[d]) == topo.chip(cores[a])][0]
 
-    def far_of(a):
-        ds = [d for d in range(N) if topo.chip(cores[d]) != topo.chip(cores[a])]
-        return sorted(ds, key=lambda d: slot_home(a, d))
+    def turn(a):
+        return 1 if (a - near_of(a)) % N == 1 else -1
 
-    far = far_of(r)
-    near = [d for d in range(N) if d != r and d not in far][0]
-    order = far + [near, r]
-    slot = [slot_home(r, d) for d in order]
+    def slot_of(home, d):
+        return (N - 1 + turn(home) * (d - home)) % N
+
+    order = sorted(range(N), key=lambda d: slot_of(r, d))
+    far, near = order[:2], order[2]
+    assert near == near_of(r) and order[3] == r
     far_eng = topo.engines(core, cores[far[0]])
     near_eng = [e for e in topo.engines(core, cores[near]) if e not in far_eng]
     half = len(far_eng) // 2
@@ -113,11 +118,15 @@ def rank_program(g, core, T, topo):
         g.remote_dma(dst, src, sem, T.sem.sent, pid, rid, near_mask)
         sent[0] += len(near_eng)
 
-    def bank(b, n):
-        return T.pp[:, 512 * b:512 * b + n]
+    def bank(b, n, c0=0):
+        return T.pp[:, 512 * b + c0:512 * b + n]
 
+    def fill(dst, n, value, t=None):
+        return done(S.activation(dst, T.ones[:, 0:n], ACT.Identity, scale=value), t)
+
+    runs = ((0, HW), (HW, TC))
     t_u = done(SY.dma_start(T.us[:], T.u[:]), k=16)
-    t_x = done(SY.dma_start(T.xs[:], T.x[:]), k=16)
+    t_x = [done(SY.dma_start(T.xs[:, 4 * j0:4 * j1], T.x[:, 4 * j0:4 * j1]), k=16) for j0, j1 in runs]
     t_a = done(SY.dma_start(b8(T.aq[:]), T.ac[:]), k=16)
     done(SY.dma_start(T.asc[:], T.ap[:]), t_a, 16)
     t_c = done(SY.dma_start(b8(T.cq[:]), T.cc[:]), k=16)
@@ -126,45 +135,34 @@ def rank_program(g, core, T, topo):
     t_v = done(SY.dma_start(T.vs[:], T.v[:]), k=16)
 
     fl_ok = {"allow_small_or_imprecise_dtypes": True}
-    t_ip = done(g.iota(T.ip[:], [[4 * (N - 1 - r), 2]], 0, 1))
+    sg = turn(r)
+    t_ip = done(g.iota(T.ip[:, 0:1], [[0, 1]], 0, 1))
+    done(g.iota(T.ip[:, 1:2], [[0, 1]], 4 * ((N - 1 - sg * r) % N) + 128, sg), t_ip)
+    t_ip2 = done(g.iota(T.ip[:, 2:3], [[0, 1]], 0, 17))
     t_ul = done(g.iota(T.ul[:], [[16, 8]], 0, 0))
-    t_i4 = done(g.iota(T.i4[:], [[0, C // 4], [1, 4]], 0, 0, **fl_ok))
-    t_vals = done(g.iota(T.vals[:], [[64, 2], [128, 10], [4, 16]], -64, 0, **fl_ok))
+    t_c152 = done(g.iota(T.c152[:], [[0, 38], [int(BIG), 4]], 0, 0, **fl_ok))
+    t_vals = done(g.iota(T.vals[:], [[-4, TC]], 4 * TC, 0, **fl_ok))
+    t_jr = done(g.iota(T.jr[:], [[16, 32]], 4 * C, 0, **fl_ok))
 
     t_ones = done(V.memset(T.ones[:], 1.0))
-    wait("S", t_ones)
-    t_z1 = done(S.activation(T.c152[:], T.ones[:, 0:152], ACT.Identity, scale=0.0))
-    t_z = done(S.activation(T.fl[:], T.ones[:, 0:TC], ACT.Identity, scale=0.0))
-    done(S.activation(T.win[:, 0:4 * C], T.ones[:, 0:4 * C], ACT.Identity, scale=0.0), t_z)
-
-    wait("G", t_ones)
-    t_e = tok()
-    for b in range(4):
-        done(g.affine_select(T.ebf[:, 512 * b:512 * b + 512], T.ones[:], [[1, 512]], OP.is_equal, 0.0, -b, -4), t_e)
-
-    ai, wi_, ti, hi, qi = [T.ci[:, k:k + 1] for k in range(5)]
-    acol, winit, hcol, sub1, c4, x1, nh, x2, sub2, qcol = [T.cf[:, k:k + 1] for k in range(10)]
+    wait("V", t_ones)
+    t_pad = done(V.tensor_copy(T.rr[:], T.ones[:]))
     wait("V", t_ip)
-    t_l1 = done(V.tensor_scalar(T.ci[:, 0:2], T.ip[:], 2, 3, OP.logical_shift_right, OP.bitwise_and))
-    done(V.tensor_scalar(ti, T.ip[:, 0:1], 3, None, OP.bitwise_and), t_l1)
-    done(V.tensor_scalar(hi, T.ip[:, 0:1], 4, 1, OP.logical_shift_right, OP.bitwise_and), t_l1)
+    t_l1 = done(V.tensor_scalar(T.ci[:, 0:2], T.ip[:, 0:2], 2, 3, OP.logical_shift_right, OP.bitwise_and))
+    done(V.tensor_scalar(T.ci[:, 2:3], T.ip[:, 0:1], 3, None, OP.bitwise_and), t_l1)
+    done(V.tensor_scalar(T.ci[:, 3:4], T.ip[:, 0:1], 15, None, OP.bitwise_and), t_l1)
+    wait("V", t_ip2)
+    done(V.tensor_scalar(T.ci[:, 4:5], T.ip[:, 2:3], 4, 1, OP.logical_shift_right, OP.bitwise_and), t_l1)
     wait("V", t_l1)
-    t_l2 = done(V.tensor_copy(acol, ai))
-    done(V.tensor_scalar(c4, hi, -5.0 * BIG, BIG, OP.mult, OP.add), t_l2)
-    done(V.tensor_scalar(x1, ai, -BIG, 3.0 * BIG, OP.mult, OP.add), t_l2)
-    t_l2b = done(V.tensor_scalar(winit, wi_, 0.25, None, OP.mult))
-    done(V.tensor_scalar(sub1, hi, -BIG, BIG + 1.0, OP.mult, OP.add), t_l2b)
+    t_l2 = done(V.tensor_copy(T.cf[:], T.ci[:]))
+    acol, wcol, tcol, qcol, pcol = [T.cf[:, k:k + 1] for k in range(5)]
+    winit, nega, top, g0, g1 = [T.cs[:, k:k + 1] for k in range(5)]
     wait("V", t_l2, t_ul)
     t_uo = done(V.tensor_scalar(T.uoff[:], T.ul[:], acol, None, OP.add))
-    t_x2 = done(V.tensor_scalar(x2, hi, -64.0, x1, OP.mult, OP.add))
-    wait("V", t_i4)
-    t_cs = done(V.tensor_scalar(T.csel[:], T.i4[:], acol, -8.0 * BIG, OP.is_equal, OP.mult))
-    wait("V", t_x2)
-    t_l4 = done(V.tensor_scalar(sub2, ti, -1.0, x2, OP.mult, OP.add))
 
-    wait("S", t_z1, t_l2)
-    done(S.activation(T.c152[:, 0:152:8], T.ones[:, 0:19], ACT.Identity, scale=-4.0 * BIG), t_z)
-    done(S.activation(T.c152[:, 4:152:8], T.ones[:, 0:19], ACT.Identity, scale=c4), t_z)
+    wait("S", t_ones)
+    t_z = fill(T.fl[:], TC, 0.0)
+    t_win = fill(T.win[:, 0:4 * C], 4 * C, 4.0)
 
     wait("V", t_u)
     t_qu = done(V.quantize_mx(T.uq[:], T.usc[:], T.us[:]))
@@ -172,124 +170,130 @@ def rank_program(g, core, T, topo):
     t_pu = done(V.tensor_copy(T.uq2[:].bitcast(dt.uint32), T.uq[:].bitcast(dt.uint32).indirect(T.uoff[:])))
     wait("S", t_qu, t_uo)
     done(S.activation(T.usc2[:], T.usc[:].indirect(T.uoff[:]), ACT.Copy), t_pu)
+    wait("PE", t_pu)
+    t_p = []
+    for n, (j0, j1) in enumerate(runs):
+        wait("V", t_x[n])
+        t_qx = done(V.quantize_mx(T.xq[:, j0:j1], T.xsc[:, j0:j1], T.xs[:, 4 * j0:4 * j1]))
+        wait("PE", t_qx)
+        t_p.append(done(PE.matmul_mx(bank(n, j1 - j0), T.uq2[:], T.usc2[:], T.xq[:, j0:j1], T.xsc[:, j0:j1],
+                                     True, True)))
 
-    wait("V", t_x)
-    t_qx = done(V.quantize_mx(T.xq[:], T.xsc[:], T.xs[:]))
-    wait("V", t_vals, t_cs)
-    t_pad = done(V.tensor_scalar(T.rr[:, 0:16], T.vals[:, 0:16], 0.25, TC + 17.0, OP.mult, OP.add))
-    done(V.tensor_scalar(T.rr[:, 304:320], T.vals[:, 0:16], 0.25, TC + 17.0, OP.mult, OP.add), t_pad)
-    done(V.tensor_scalar(T.csel[:], T.csel[:], BIG, None, OP.add), t_l4)
+    wait("S", t_l2)
+    t_s1 = done(S.activation(winit, wcol, ACT.Identity, scale=0.25))
+    t_s2 = done(S.activation(g0, pcol, ACT.Identity, scale=-76.0, bias=83.0))
+    done(S.activation(nega, acol, ACT.Identity, scale=-BIG), t_s2)
+    t_s3 = done(S.activation(top, tcol, ACT.Identity, bias=4.0 * TC))
+    wait("S", t_s2, t_c152)
+    t_g1 = done(S.activation(g1, qcol, ACT.Identity, scale=4.0, bias=g0))
+    done(S.activation(T.csel[:], T.c152[:, 0:C], ACT.Relu, bias=nega), t_s3)
+    t_ez = tok()
+    for c0 in range(0, 2048, 256):
+        fill(T.ebf[:, c0:c0 + 256], 256, 0.0, t_ez)
+    wait("G", t_ones, t_ez)
+    t_e = tok()
+    for b in range(4):
+        done(g.affine_select(T.ebf[:, 512 * b + b:512 * b + 512:4], T.ones[:, 0:128], [[1, 128]], OP.is_equal, 0.0,
+                             0, -1), t_e)
+    t_hp = fill(T.hn[:, 0:4 * PAD], 4 * PAD, 0.0)
+    t_d = fill(T.d0[:, 0:64:2], 32, BIG)
+    wait("S", t_jr)
+    done(S.activation(T.d1[:, 1:64:2], T.jr[:], ACT.Identity, bias=qcol), t_d)
+    t_xw = tok()
+    for b in RAW:
+        fill(T.dw[:, DW * b + 4 * C:DW * (b + 1)], TC, 0.0, t_xw)
+    wait("S", *t_x)
+    for b in SUM:
+        done(S.activation(T.dw[:, DW * b + 4 * C:DW * (b + 1)], T.xs[:, b:4 * TC:4], ACT.Copy), t_xw)
 
-    wait("PE", t_pu, t_qx)
-    t_p = done(PE.matmul_mx(bank(0, TC), T.uq2[:], T.usc2[:], T.xq[:], T.xsc[:], True, True))
-
-    wait("V", t_z, t_l2b, t_pad, t_l4, t_p)
-    t_pt = done(V.transpose(T.pt[:], bank(0, TC)))
-    wait("V", t_pt)
+    tv = tok()
+    for n, (j0, j1) in enumerate(runs):
+        wait("V", t_p[n])
+        done(V.transpose(T.pt[:, j0:j1], bank(n, j1 - j0)), tv)
+    wait("V", tv)
     ev, od = T.pt[:, 0:TC:8], T.pt[:, 4:TC:8]
     t1 = done(V.tensor_tensor(T.mm[:], ev, od, OP.max))
-    t2 = done(V.tensor_tensor(T.ww[:], ev, od, OP.is_ge))
+    done(V.tensor_tensor(T.ww[:], ev, od, OP.is_ge), tv)
     wait("V", t1)
-    done(V.tensor_tensor(T.ff[:, 0:36:2], T.mm[:, 0:36:2], T.mm[:, 1:36:2], OP.is_ge), t2)
-    done(V.tensor_tensor(T.ff[:, 1:36:2], T.mm[:, 0:36:2], T.mm[:, 1:36:2], OP.is_lt), t2)
-    wait("V", t2)
-    t3 = done(V.tensor_tensor(T.fl[:, 0:TC:8], T.ff[:], T.ww[:], OP.mult))
-    done(V.tensor_tensor(T.fl[:, 4:TC:8], T.ff[:], T.ww[:], OP.is_gt), t3)
-    wait("V", t3)
-    t4 = done(V.transpose(T.fr[:], T.fl[:]))
-    wait("V", t4)
-    t5 = done(V.tensor_tensor_scan(T.cum[:], T.fr[:], T.fr[:], winit, OP.add, OP.max))
-    wait("V", t5)
-    t6 = done(V.tensor_tensor_scan(T.rr[:, 16:304], T.cum[:], T.fr[:], 0.0, OP.max, OP.mult))
-    wait("V", t6)
-    t7 = done(V.transpose(T.tt[:, 0:320], T.rr[:, 0:320]))
-    done(V.transpose(T.tt[:, 320:608], T.rr[:, 16:304]), t7)
-    wait("V", t7)
-    t8 = done(V.tensor_tensor_scan(T.s152[:], T.c152[:], T.tt[:, 0:608:4], 0.0, OP.add, OP.max))
-    wait("V", t8)
-    t9 = done(V.tensor_scalar(T.loff[:, 0:19], T.s152[:, 7:152:8], sub1, 4.0, OP.subtract, OP.mult))
-    wait("V", t9)
-    t10 = done(V.tensor_copy(T.win[:].indirect(T.loff[:, 0:19]), T.vals[:, 0:304]))
-    wait("V", t10)
+    done(V.tensor_tensor(T.ff[:, 0:36:2], T.mm[:, 0:36:2], T.mm[:, 1:36:2], OP.is_ge), tv)
+    done(V.tensor_tensor(T.ff[:, 1:36:2], T.mm[:, 0:36:2], T.mm[:, 1:36:2], OP.is_lt), tv)
+    wait("V", tv, t_z)
+    done(V.tensor_tensor(T.fl[:, 0:TC:8], T.ff[:], T.ww[:], OP.mult), tv)
+    done(V.tensor_tensor(T.fl[:, 4:TC:8], T.ff[:], T.ww[:], OP.is_gt), tv)
+    wait("V", tv)
+    done(V.transpose(T.fr[:], T.fl[:]), tv)
+    wait("V", t_g1, t_s1)
+    t_gl = done(V.tensor_scalar(T.gl[:], T.ul[:, 0:5:4], g1, 151.0, OP.add, OP.min))
+    wait("V", tv)
+    done(V.tensor_tensor_scan(T.cum[:], T.fr[:], T.fr[:], winit, OP.add, OP.max), tv)
+    wait("V", tv, t_pad)
+    done(V.tensor_tensor_scan(T.rr[:, 16:304], T.cum[:], T.fr[:], 0.0, OP.max, OP.mult), tv)
+    wait("V", tv)
+    done(V.transpose(T.tt[:, 0:320], T.rr[:, 0:320]), tv)
+    done(V.transpose(T.tt[:, 320:608], T.rr[:, 16:304]), tv)
+    wait("V", tv, t_c152)
+    t8 = done(V.tensor_tensor_scan(T.s152[:], T.c152[:], T.tt[:, 0:608:4], 0.0, OP.min, OP.max))
+    wait("V", t8, t_gl)
+    places = T.s152[:].indirect(T.gl[:])
+    done(V.tensor_scalar(T.loff[:], places, 4.0, -4.0, OP.mult, OP.add), tv)
+    wait("V", tv, t_win, t_vals)
+    done(V.tensor_copy(T.win[:].indirect(T.loff[:, 0:NL]), T.vals[:]), tv)
 
-    def select(lo):
-        t = tok()
-        for i in (lo, lo + 1):
-            done(V.tensor_tensor_scan(T.sel[:, C * i:C * i + C], T.csel[:], T.win[:, slot[i]:4 * C:4], 0.0,
-                                      OP.add, OP.max), t)
-        wait("V", t)
-        return done(V.tensor_scalar(T.goff[:, 20 * lo:20 * lo + 40], T.sel[:, C * lo + 3:C * lo + HW:4], sub2, None,
-                                    OP.subtract))
+    wait("S", t8, t_gl)
+    done(S.activation(T.d1[:, 0:64:2], places, ACT.Identity, scale=4.0, bias=-4.0), t_d)
+    done(S.activation(T.d0[:, 1:64:2], places, ACT.Relu, scale=4.0 * BIG, bias=-(4.0 * C + 3.5) * BIG), t_d)
+
+    wait("V", tv, t_s3)
+
+    def select(i, t=None):
+        return done(V.tensor_tensor_scan(T.sel[:, C * i:C * i + C], T.csel[:], T.win[:, i:4 * C:4], 0.0,
+                                         OP.min, OP.max), t)
+
+    def offsets(lo):
+        return done(V.tensor_scalar(T.goff[:, 20 * lo:20 * lo + 40], T.sel[:, C * lo + 3:C * lo + HW:4], -1.0, top,
+                                    OP.mult, OP.add))
 
     def gather(q, dst, src, t=None):
         if q == "V":
             return done(V.tensor_copy(dst, src), t)
         return done(S.activation(dst, src, ACT.Copy), t)
 
-    def bundle(q, i, t=None):
-        return gather(q, T.xb[:, 4 * C * slot[i]:4 * C * (slot[i] + 1)],
-                      T.xs[:].indirect(T.goff[:, 20 * i:20 * i + 20]), t)
+    def bundle(q, c0, c1, t=None):
+        return gather(q, T.xb[:, 16 * c0:16 * c1], T.xs[:].indirect(T.goff[:, c0:c1]), t)
 
-    t_ga = select(0)
+    select(0, tv)
+    select(1, tv)
+    t_s23 = select(2)
+    wait("V", tv)
+    t_ga = offsets(0)
+    select(3, t_s23)
     wait("V", t_ga)
-    t_b01 = bundle("V", 0)
-    wait("S", t_x, t_ga)
-    bundle("S", 1, t_b01)
+    t_b01 = bundle("V", 0, 18)
+    wait("S", t_ga)
+    bundle("S", 18, 40, t_b01)
+    wait("V", t_s23)
+    t_gb = offsets(2)
     wait("V", t_b01)
-    t_q1 = done(V.quantize_mx(T.qa[:], T.sa[:], T.xb[:, 4 * C * slot[0]:4 * C * slot[0] + 4 * HW]))
-    t_gb = select(2)
-    wait("V", t_gb)
-    t_b2 = bundle("V", 2)
+    t_q1 = done(V.quantize_mx(T.qa[:], T.sa[:], T.xb[:, 0:4 * HW]))
     wait("S", t_gb)
-    t_b3 = bundle("S", 3)
-    wait("V", t_b2)
-    n0 = max(0, C * slot[2] + C - 128)
-    nb = C * slot[2] - n0
-    t_q2 = done(V.quantize_mx(T.qb[:], T.sb[:], T.xb[:, 4 * n0:4 * (n0 + 128)]))
-    wait("V", t_b3)
-    t_q3 = done(V.quantize_mx(T.lb[:, 0:128], T.lbs[:, 0:128], T.xb[:, 4 * (4 * C - 128):4 * 4 * C]))
+    t_b23 = bundle("S", 40, 64)
+    wait("V", t_gb)
+    bundle("V", 64, 80, t_b23)
+    wait("V", t_b23)
+    t_q2 = done(V.quantize_mx(T.qb[:, 0:HW], T.sb[:, 0:HW], T.xb[:, 4 * HW:8 * HW]))
 
-    at = [C * far_of(d).index(r) for d in far]
+    at = [C * slot_of(d, r) for d in far]
     wait("G", t_q1)
     send_far([b8(T.qa[:, C * i:C * i + C]) for i in range(2)], [b8(T.la[:, a:a + C]) for a in at], T.sem.arr_far)
     send_far([T.sa[:, C * i:C * i + C] for i in range(2)], [T.las[:, a:a + C] for a in at], T.sem.arr_far)
     wait("G", t_q2)
-    send_near(b8(T.qb[:, nb:nb + C]), b8(T.lb[:, 128:128 + C]), T.sem.arr_near)
-    send_near(T.sb[:, nb:nb + C], T.lbs[:, 128:128 + C], T.sem.arr_near)
+    send_near(b8(T.qb[:, 0:C]), b8(T.qb[:, HW:HW + C]), T.sem.arr_near)
+    send_near(T.sb[:, 0:C], T.sb[:, HW:HW + C], T.sem.arr_near)
 
-    t_jr = done(g.iota(T.jr[:], [[16, 18]], 4 * C, 0, **fl_ok))
-    n_hi = 4 * C - C * (r + 1)
     t_tab = tok()
-    if n_hi:
-        done(g.iota(T.tab[:, 0:n_hi], [[1, n_hi]], C * (r + 1), 0, **fl_ok), t_tab)
-    done(g.iota(T.tab[:, n_hi:4 * C], [[1, 4 * C - n_hi]], 0, 0, **fl_ok), t_tab)
-    t_xw = tok()
-    for b in range(4):
-        done(S.activation(T.dw[:, DW * b + 4 * C:DW * (b + 1)], T.xs[:, b:4 * TC:4], ACT.Copy), t_xw)
-    done(S.activation(T.tab[:, 4 * C:DW], T.ones[:, 0:TC], ACT.Identity, scale=-1.0), t_tab)
-
-    h1 = done(V.tensor_scalar(T.zz[:, 0:19:2], T.s152[:, 7:80:8], sub1, 4.0, OP.subtract, OP.mult))
-    done(V.tensor_scalar(T.zz[:, 1:19:2], T.s152[:, 87:152:8], sub1, 4.0, OP.subtract, OP.mult), h1)
-    done(V.tensor_copy(hcol, hi), h1)
-    done(V.tensor_scalar(nh, hi, -1.0, 1.0, OP.mult, OP.add), h1)
-    done(V.tensor_scalar(qi, T.ip[:, 0:1], 15, None, OP.bitwise_and), h1)
-    wait("V", h1)
-    h2 = done(V.tensor_scalar(T.n1[:], T.zz[:, 1:19], nh, None, OP.mult))
-    done(V.tensor_scalar(T.n2[:], T.zz[:, 0:18], hcol, None, OP.mult), h2)
-    done(V.tensor_copy(qcol, qi), h2)
-    wait("V", h2)
-    h3 = done(V.tensor_tensor(T.ni[:], T.n1[:], T.n2[:], OP.add))
-    wait("V", h3)
-    h4 = done(V.tensor_scalar(T.wi[:], T.ni[:], 3, None, OP.bitwise_and))
-    done(V.tensor_scalar(T.ki[:], T.ni[:], 2, None, OP.logical_shift_right), h4)
-    done(V.tensor_scalar(T.ov[:], T.ni[:], 4.0 * C, BIG, OP.is_ge, OP.mult), h4)
-    wait("V", h4)
-    h5 = done(V.tensor_scalar(T.w80[:], T.wi[:], float(C), None, OP.mult))
-    done(V.tensor_tensor(T.s1[:], T.ki[:], T.ov[:], OP.add), h5)
-    wait("V", h5)
-    h6 = done(V.tensor_tensor(T.s2[:], T.s1[:], T.w80[:], OP.add))
-    wait("V", t_e)
-    t_qe = done(V.quantize_mx(T.eq[:], T.esc[:], T.ebf[:]))
+    for s, d in enumerate(order):
+        done(g.iota(T.tab[:, s:4 * C:4], [[1, C]], C * d, 0, **fl_ok), t_tab)
+    done(g.iota(T.tab[:, 4 * C:DW], [[0, TC]], -1, 0, **fl_ok), t_tab)
 
     def relu(q, dst, src, t):
         if q == "V":
@@ -301,124 +305,206 @@ def rank_program(g, core, T, topo):
             return done(V.tensor_scalar(dst, src, 0.0625, None, OP.mult), t)
         return done(S.activation(dst, src, ACT.Identity, scale=0.0625), t)
 
-    def layer(q, s, i, b0, mq, ms, start, stop):
-        ts = []
-        for b in range(4):
-            k = 512 * i + 128 * b
-            ins = PE.matmul_mx(bank(b0 + b, HW), q[:, k:k + 128], s[:, k:k + 128], mq, ms, start, stop)
-            ts.append(done(ins) if stop else None)
-        return ts
+    def product(q, s, i, b, b0, m, start, stop):
+        k = 512 * i + 128 * b
+        ins = PE.matmul_mx(bank(b0 + b, m[2]), q[:, k:k + 128], s[:, k:k + 128], m[0], m[1], start, stop)
+        return done(ins) if stop else None
 
-    def htile(hf, i):
-        n = 2 * hf + i
-        return 4 * HW * n, T.hq[:, HW * n:HW * n + HW], T.hs[:, HW * n:HW * n + HW]
+    def layer_a(i, b0, m):
+        return [product(T.aq, T.asc, i, b, b0, m, True, True) for b in range(4)]
 
-    def evict(fn, buf, o, b0, ts, who, t):
-        for q, b in who:
+    def layer_c(i, b0, m):
+        return [product(T.cq, T.csc, i, b, b0, m, i == 0, i == 1) for b in range(4)]
+
+    def width(p):
+        return HW if p == "f" else 128
+
+    def tile_out(p, n, b):
+        if p == "f":
+            return T.hf[:, 4 * HW * n + b:4 * HW * (n + 1):4]
+        c0 = PAD + C * (n + (3 if p == "n" else 0))
+        return T.hn[:, 4 * c0 + b:4 * (c0 + C):4]
+
+    def tile_in(p, n):
+        if p == "f":
+            return T.hf[:, 4 * HW * n:4 * HW * (n + 1)]
+        c0 = C * (n + (3 if p == "n" else 0))
+        return T.hn[:, 4 * c0:4 * (c0 + 128)]
+
+    def packed(p, n):
+        w = width(p)
+        if n < 2:
+            c0 = {"f": HW * n, "o": 2 * HW + 128 * n, "n": 2 * HW + 256 + 128 * n}[p]
+            return T.hq[:, c0:c0 + w], T.hs[:, c0:c0 + w], w
+        c0 = {"f": 0, "o": HW, "n": HW + 128}[p]
+        return T.zq[:, c0:c0 + w], T.zs[:, c0:c0 + w], w
+
+    ev_tok = {}
+
+    def evict(q, p, n, b0, ts, bs):
+        t = ev_tok.setdefault((p, n), None) or tok()
+        ev_tok[p, n] = t
+        for b in bs:
             wait(q, ts[b])
-            fn(q, buf[:, o + b:o + 4 * HW:4], bank(b0 + b, HW), t)
+            (relu if n < 2 else scaled)(q, tile_out(p, n, b), bank(b0 + b, width(p), 0 if p == "f" else PAD), t)
+        return t
 
-    def expert(hf, mq, ms, bx, by, free_y):
-        o0, q0, s0 = htile(hf, 0)
-        o1, q1, s1 = htile(hf, 1)
-        ta0 = layer(T.aq, T.asc, 0, bx, mq, ms, True, True)
-        wait("PE", *free_y)
-        ta1 = layer(T.aq, T.asc, 1, by, mq, ms, True, True)
-        e0, e1, ez = tok(), tok(), tok()
-        evict(relu, T.hb, o0, bx, ta0, (("V", 0), ("S", 1), ("V", 2), ("S", 3)), e0)
-        wait("V", e0)
-        th0 = done(V.quantize_mx(q0, s0, T.hb[:, o0:o0 + 4 * HW]))
-        evict(relu, T.hb, o1, by, ta1, (("S", 0), ("S", 1), ("V", 2), ("S", 3)), e1)
-        wait("V", e1)
-        th1 = done(V.quantize_mx(q1, s1, T.hb[:, o1:o1 + 4 * HW]))
-        wait("PE", t_c, th0)
-        layer(T.cq, T.csc, 0, bx, q0, s0, True, False)
-        wait("PE", th1)
-        tc = layer(T.cq, T.csc, 1, bx, q1, s1, False, True)
-        oz = 4 * HW * hf
-        evict(scaled, T.zb, oz, bx, tc, (("V", 0), ("S", 1), ("V", 2), ("S", 3)), ez)
-        wait("V", ez)
-        return done(V.quantize_mx(T.zq[:, HW * hf:HW * hf + HW], T.zs[:, HW * hf:HW * hf + HW],
-                                  T.zb[:, oz:oz + 4 * HW]))
+    def quantise(p, n):
+        wait("V", ev_tok[p, n])
+        q, s, _w = packed(p, n)
+        return done(V.quantize_mx(q, s, tile_in(p, n)))
 
-    wait("PE", t_pt, t_a, t_q3)
+    def quantise_e(b0, b1, t=None):
+        return done(V.quantize_mx(T.eq[:, 128 * b0:128 * b1], T.esc[:, 128 * b0:128 * b1],
+                                  T.ebf[:, 512 * b0:512 * b1]), t)
+
+    mo = (T.qb[:, HW - 128:HW], T.sb[:, HW - 128:HW], 128)
+    wait("PE", tv, t_a, t_q2)
+    o0 = layer_a(0, 0, mo)
+    o1 = layer_a(1, 4, mo)
+    wait("V", t_d)
+    done(V.tensor_tensor_scan(T.d2[:], T.d0[:], T.d1[:], 0.0, OP.add, OP.min), tv)
+    evict("S", "o", 0, 0, o0, (0, 1, 2))
+    evict("V", "o", 0, 0, o0, (3,))
+    wait("V", tv)
+    t_h = done(V.tensor_copy(T.hoff[:], T.d2[:, 1:2 * NL:2]))
+    wait("V", t_hp)
+    q_o0 = quantise("o", 0)
+    evict("S", "o", 1, 4, o1, (0, 1, 2))
+    evict("V", "o", 1, 4, o1, (3,))
+    q_o1 = quantise("o", 1)
+    wait("V", t_e)
+    t_qe = quantise_e(0, 2)
+    wait("PE", t_c, q_o0)
+    layer_c(0, 0, packed("o", 0))
+    wait("PE", q_o1)
+    oc_ = layer_c(1, 0, packed("o", 1))
+    evict("S", "o", 2, 0, oc_, (0, 1, 2))
+    evict("V", "o", 2, 0, oc_, (3,))
+    q_oz = quantise("o", 2)
+    quantise_e(2, 4, t_qe)
+
+    mf = (T.la[:], T.las[:], HW)
+    mn = (T.qb[:, 3 * C - 128:3 * C], T.sb[:, 3 * C - 128:3 * C], 128)
     PE.wait_ge(T.sem.arr_far, 4 * half)
-    t_za = expert(0, T.la[:], T.las[:], 0, 4, [])
+    f0 = layer_a(0, 4, mf)
+    wait("PE", ev_tok["o", 2])
+    f1 = layer_a(1, 0, mf)
+    evict("V", "f", 0, 4, f0, (0, 2))
+    evict("S", "f", 0, 4, f0, (1, 3))
+    q_f0 = quantise("f", 0)
+    evict("S", "f", 1, 0, f1, (0, 1, 3))
+    evict("V", "f", 1, 0, f1, (2,))
+    q_f1 = quantise("f", 1)
+    wait("PE", ev_tok["f", 0])
     PE.wait_ge(T.sem.arr_near, 2 * len(near_eng))
-    t_zb = expert(1, T.lb[:, 128 - C:128 + C], T.lbs[:, 128 - C:128 + C], 4, 0, [t_za])
+    n0 = layer_a(0, 4, mn)
+    wait("PE", q_f0, ev_tok["f", 1])
+    layer_c(0, 0, packed("f", 0))
+    wait("PE", q_f1)
+    fc = layer_c(1, 0, packed("f", 1))
+    evict("S", "n", 0, 4, n0, (0, 1, 2, 3))
+    wait("PE", ev_tok["n", 0])
+    n1 = layer_a(1, 4, mn)
+    q_n0 = quantise("n", 0)
+    evict("V", "f", 2, 0, fc, (0, 2))
+    evict("S", "f", 2, 0, fc, (1, 3))
+    q_fz = quantise("f", 2)
+    evict("S", "n", 1, 4, n1, (0, 1, 2))
+    evict("V", "n", 1, 4, n1, (3,))
+    q_n1 = quantise("n", 1)
+    wait("PE", q_n0, ev_tok["f", 2])
+    layer_c(0, 0, packed("n", 0))
+    wait("PE", q_n1)
+    nc = layer_c(1, 0, packed("n", 1))
+    evict("V", "n", 2, 0, nc, (0, 2))
+    evict("S", "n", 2, 0, nc, (1, 3))
+    q_nz = quantise("n", 2)
 
-    hm = [C * slot_home(d, r) for d in far]
-    wait("G", t_za)
-    send_far([b8(T.zq[:, C * i:C * i + C]) for i in range(2)], [b8(T.zl[:, a:a + C]) for a in hm], T.sem.home)
-    send_far([T.zs[:, C * i:C * i + C] for i in range(2)], [T.zls[:, a:a + C] for a in hm], T.sem.home)
-    hn = C * slot_home(near, r)
-    wait("G", t_zb)
-    send_near(b8(T.zq[:, 3 * C:4 * C]), b8(T.zl[:, hn:hn + C]), T.sem.home)
-    send_near(T.zs[:, 3 * C:4 * C], T.zls[:, hn:hn + C], T.sem.home)
+    wait("G", q_fz)
+    send_far([b8(T.zq[:, C * a:C * a + C]) for a in range(2)], [b8(T.zl[:, a:a + C]) for a in at], T.sem.home_far)
+    send_far([T.zs[:, C * a:C * a + C] for a in range(2)], [T.zls[:, a:a + C] for a in at], T.sem.home_far)
+    zn = HW + 128 + PAD
+    wait("G", q_nz)
+    send_near(b8(T.zq[:, zn:zn + C]), b8(T.zl[:, HW:HW + C]), T.sem.home_near)
+    send_near(T.zs[:, zn:zn + C], T.zls[:, HW:HW + C], T.sem.home_near)
 
-    def decode(b0, mq, ms, n, keep, c0, ts):
-        out = []
+    def decode(b0, m, slots, ts):
         for b in range(4):
-            t = done(PE.matmul_mx(bank(b0 + b, n), T.eq[:, 128 * b:128 * b + 128], T.esc[:, 128 * b:128 * b + 128],
-                                  mq, ms, True, True))
-            wait("V", t)
-            out.append(done(V.tensor_tensor(T.dw[:, DW * b + c0:DW * b + c0 + keep], bank(b0 + b, keep),
-                                            T.xb[:, 4 * c0 + b:4 * (c0 + keep):4], OP.add), ts))
-        return out
+            t = done(PE.matmul_mx(bank(b0 + b, m[2]), T.eq[:, 128 * b:128 * b + 128],
+                                  T.esc[:, 128 * b:128 * b + 128], m[0], m[1], True, True))
+            for k, s in enumerate(slots):
+                c0 = m[2] - C * (len(slots) - k)
+                dst, src = T.dw[:, DW * b + s:DW * b + 4 * C:4], bank(b0 + b, c0 + C, c0)
+                if b in RAW:
+                    wait("S", t)
+                    done(S.activation(dst, src, ACT.Copy), ts[b])
+                else:
+                    wait("V", t)
+                    done(V.tensor_tensor(dst, src, T.xb[:, 4 * C * s + b:4 * C * (s + 1):4], OP.add), ts[b])
 
-    wait("V", h6, t_jr)
-    h7 = done(V.tensor_scalar(T.jt[:], T.jr[:], qcol, None, OP.add))
-    wait("V", h7)
-    h8 = done(V.tensor_tensor(T.s3[:], T.s2[:], T.jt[:], OP.min))
-    wait("V", h8)
-    t_h = done(V.tensor_copy(T.hoff[:], T.s3[:]))
-    wait("PE", t_qe, t_zb)
-    t_own = tok()
-    decode(0, T.zq[:, HW:HW + 128], T.zs[:, HW:HW + 128], 128, C, 3 * C, t_own)
+    t_own, t_far = tok(), tok()
+    wait("PE", t_qe, q_oz, ev_tok["n", 1])
+    decode(4, packed("o", 2), (3,), [t_own] * 4)
     wait("V", t_v)
     t_qv = done(V.quantize_mx(T.vq[:], T.vsc[:], T.vs[:]))
-
     wait("S", t_h, t_tab)
     t_olr = done(S.activation(T.olr[:], T.tab[:].indirect(T.hoff[:]), ACT.Copy))
     wait("SY", t_olr)
     t_out = done(SY.dma_start(T.ol[:], T.olr[0:128:16, :]), k=16)
 
-    wait("PE", t_own, t_qv)
-    wait("V", t_h, t_own, t_xw)
-    wait("S", t_own, t_xw)
-    PE.wait_ge(T.sem.home, 4 * half + 2 * len(near_eng))
-    t_d = decode(4, T.zl[:], T.zls[:], 3 * C, 3 * C, 0, None)
+    wait("PE", ev_tok["n", 2])
+    PE.wait_ge(T.sem.home_far, 4 * half)
+    decode(0, (T.zl[:, 0:HW], T.zls[:, 0:HW], HW), (0, 1), [t_far] * 4)
+    wait("PE", t_own)
+    PE.wait_ge(T.sem.home_near, 2 * len(near_eng))
+    t_dn = [tok() for b in range(4)]
+    decode(4, (T.zl[:, 3 * C - 128:3 * C], T.zls[:, 3 * C - 128:3 * C], 128), (2,), t_dn)
+    wait("V", t_h, t_own, t_far, t_xw)
+    wait("S", t_own, t_far, t_xw)
+    wait("PE", t_far, t_qv)
 
-    runs = ((0, HW), (HW, TC))
-    who = (("S", "S", "S", "V"), ("S", "S", "V", "V"))
     ty = [tok(), tok()]
 
-    def pick_y(q, n):
+    def pick_y(n, b):
         j0, j1 = runs[n]
-        for b in (range(4) if q == "S" else range(3, -1, -1)):
-            if who[n][b] == q:
-                wait(q, t_d[b])
-                gather(q, T.yb[:, 4 * j0 + b:4 * j1:4],
-                       T.dw[:, DW * b:DW * (b + 1)].indirect(T.hoff[:, j0 // 16:j1 // 16]), ty[n])
+        dst = T.yb[:, 4 * j0 + b:4 * j1:4]
+        src = T.dw[:, DW * b:DW * (b + 1)].indirect(T.hoff[:, j0 // 16:j1 // 16])
+        if b in RAW:
+            wait("V", t_dn[b])
+            done(V.tensor_tensor(dst, src, T.xs[:, 4 * j0 + b:4 * j1:4], OP.add), ty[n])
+        else:
+            wait("S", t_dn[b])
+            gather("S", dst, src, ty[n])
 
-    pick_y("S", 0)
-    pick_y("S", 1)
+    for n in range(2):
+        for b in SUM:
+            pick_y(n, b)
+    tq, tm = [None, None], [None, None]
     for n, (j0, j1) in enumerate(runs):
-        pick_y("V", n)
+        for b in RAW:
+            pick_y(n, b)
         wait("V", ty[n])
-        tq = done(V.quantize_mx(T.yq[:, j0:j1], T.ysc[:, j0:j1], T.yb[:, 4 * j0:4 * j1]))
-        wait("PE", tq)
-        tm = done(PE.matmul_mx(bank(n, j1 - j0), T.vq[:], T.vsc[:], T.yq[:, j0:j1], T.ysc[:, j0:j1], True, True))
-        wait("S", tm)
-        te = done(S.activation(T.yo[:, j0:j1], bank(n, j1 - j0), ACT.Copy))
-        wait("S", te)
-        done(S.dma_start(T.y[:, j0:j1], T.yo[:, j0:j1]), t_out, 16)
-        wait("SY", tq)
+        tq[n] = done(V.quantize_mx(T.yq[:, j0:j1], T.ysc[:, j0:j1], T.yb[:, 4 * j0:4 * j1]))
+        wait("PE", tq[n])
+        tm[n] = done(PE.matmul_mx(bank(n, j1 - j0), T.vq[:], T.vsc[:], T.yq[:, j0:j1], T.ysc[:, j0:j1], True, True))
+        wait("SY", tq[n])
         done(SY.dma_start(T.oc[:, 4 * j0:4 * j1], b8(T.yq[:, j0:j1])), t_out, 16)
+    wait("S", tm[0])
+    te0 = done(S.activation(T.yo[:, 0:HW], bank(0, HW), ACT.Copy))
+    wait("S", te0)
+    done(S.dma_start(T.y[:, 0:HW], T.yo[:, 0:HW]), t_out, 16)
+    wait("V", tm[1])
+    te1 = done(V.tensor_copy(T.yo[:, HW:TC], bank(1, TC - HW)))
+    wait("S", *tq)
     for k in range(4):
-        done(SY.dma_start(T.osc[4 * k:4 * k + 4, :], T.ysc[32 * k:32 * k + 4, :]), t_out, 16)
+        q = SY if k < 1 else S
+        done(q.dma_start(T.osc[4 * k:4 * k + 4, :], T.ysc[32 * k:32 * k + 4, :]), t_out, 16)
+    wait("SY", te1)
+    done(SY.dma_start(T.y[:, HW:TC], T.yo[:, HW:TC]), t_out, 16)
 
     g.wait_ge(T.sem.sent, sent[0])
     for t in toks:
-        if not t["w"] and t["n"]:
-            wait("SY", t)
+        if t is not t_out and max(list(t["w"].values()) + [0]) < t["n"]:
+            wait("G", t)
+    wait("SY", t_out)

@@ -1,16 +1,20 @@
 from concourse.bass import DstId, RemoteDMATransfer
 from concourse.mybir import dt, AluOpType, ActivationFunctionType
 
+CFG = {"near": 4, "nearh": 4, "far": 8, "late": 3, "raw": (0,), "g0": 10, "g12": 16, "g3": 8, "pe": "FA0 FA1 WA0 WA1 1C 2C0 2C1", "v": "eF0:13 qF0 eF1:3 qF1 eW0:13 qW0 eW1:3 qW1 e12:3 q12 E02 e22:13 q22", "s": "eF0:02 eF1:012 eW0:02 eW1:012 e12:012 e22:02", "dec": (1, 0, 2, 3), "yv": ((3, 0, 6), (3, 10, 12)), "vo": "E24 eo2:3 qo2", "so": "eo2:012"}
+
 N, TC, C = 4, 288, 80
 HW = 2 * C
 PAD = 128 - C
+LW = PAD + 4 * C
 DW = 4 * C + TC
 BIG = 2048.0
+HUGE = 512 * BIG
 NL = TC // 16
 Q4, U8, BF, F32, I32, U16 = "float8_e4m3fn_x4", "uint8", "bfloat16", "float32", "int32", "uint16"
 F16 = "float16"
-RAW = (0, 2)
-SUM = (1, 3)
+RAW = CFG["raw"]
+SUM = tuple(b for b in range(4) if b not in RAW)
 
 
 def _sb(n, d):
@@ -23,26 +27,23 @@ SCRATCH = {
     "xq": _sb(TC, Q4), "xsc": _sb(TC, U8),
     "uq": _sb(128, Q4), "usc": _sb(128, U8), "uq2": _sb(128, Q4), "usc2": _sb(128, U8),
     "vq": _sb(128, Q4), "vsc": _sb(128, U8),
-    "ones": _sb(320, BF), "ebf": _sb(2048, BF), "eq": _sb(512, Q4), "esc": _sb(512, U8),
+    "ones": _sb(512, BF), "ebf": _sb(2048, BF), "eq": _sb(512, Q4), "esc": _sb(512, U8),
     "ip": _sb(3, I32), "ci": _sb(5, I32), "cf": _sb(5, F32), "cs": _sb(5, F32), "ul": _sb(8, I32),
     "uoff": _sb(8, U16), "gl": _sb(2, U16),
     "csel": _sb(C, F32), "c152": _sb(152, F32), "vals": _sb(TC, F32),
     "pt": _sb(TC, F32), "mm": _sb(36, F32), "ww": _sb(36, F32), "ff": _sb(36, F32),
     "fl": _sb(TC, BF), "fr": _sb(TC, BF), "cum": _sb(TC, F16), "rr": _sb(320, F16), "tt": _sb(608, F16),
     "s152": _sb(152, F32), "loff": _sb(32, U16), "win": _sb(4 * TC, F32), "sel": _sb(4 * C, F32),
-    "goff": _sb(C, U16), "xb": _sb(16 * C, BF),
-    "qa": _sb(HW, Q4), "sa": _sb(HW, U8), "qb": _sb(3 * C, Q4), "sb": _sb(3 * C, U8),
-    "la": _sb(HW, Q4), "las": _sb(HW, U8),
-    "hf": _sb(12 * HW, BF), "hn": _sb(4 * (PAD + 6 * C), BF),
-    "hq": _sb(2 * HW + 4 * 128, Q4), "hs": _sb(2 * HW + 4 * 128, U8),
-    "zq": _sb(HW + 2 * 128, Q4), "zs": _sb(HW + 2 * 128, U8),
-    "zl": _sb(3 * C, Q4), "zls": _sb(3 * C, U8),
-    "jr": _sb(32, F32), "d0": _sb(64, F32), "d1": _sb(64, F32), "d2": _sb(64, F32),
+    "goff": _sb(C, U16), "xb": _sb(4 * LW, BF),
+    "oq": _sb(128 + HW, Q4), "op": _sb(128 + HW, U8), "lq": _sb(LW, Q4), "lp": _sb(LW, U8),
+    "hb": _sb(8 * LW, BF), "hq": _sb(2 * LW, Q4), "hp": _sb(2 * LW, U8),
+    "zb": _sb(4 * LW, BF), "zq": _sb(2 * HW, Q4), "zp": _sb(2 * HW, U8), "zl": _sb(LW, Q4), "zlp": _sb(LW, U8),
+    "jr": _sb(32, F32), "d0": _sb(96, F32), "d1": _sb(96, F32), "d2": _sb(3 * NL, F32), "rb": _sb(32, BF),
     "hoff": _sb(NL, U16), "tab": _sb(DW, F32), "olr": _sb(TC, F32),
     "dw": _sb(4 * DW, BF), "yb": _sb(4 * TC, BF), "yq": _sb(TC, Q4), "ysc": _sb(TC, U8), "yo": _sb(TC, F32),
     "pp": ("psum", [128, 4096], F32),
 }
-SEMAPHORES = ["arr_far", "arr_near", "home_far", "home_near", "sent"] + ["s%d" % i for i in range(145)]
+SEMAPHORES = ["out1", "out2", "home1", "home2", "sent"] + ["s%d" % i for i in range(145)]
 
 OP = AluOpType
 ACT = ActivationFunctionType
@@ -69,54 +70,44 @@ def rank_program(g, core, T, topo):
         t["n"] += k
         return t
 
+    def wait_for(q, t, n):
+        if t["w"].get(q, 0) < n:
+            queues[q].wait_ge(t["sem"], n)
+            t["w"][q] = n
+
     def wait(q, *ts):
         for t in ts:
-            if t["w"].get(q, 0) < t["n"]:
-                queues[q].wait_ge(t["sem"], t["n"])
-                t["w"][q] = t["n"]
+            wait_for(q, t, t["n"])
 
-    def near_of(a):
-        return [d for d in range(N) if d != a and topo.chip(cores[d]) == topo.chip(cores[a])][0]
-
-    def turn(a):
-        return 1 if (a - near_of(a)) % N == 1 else -1
-
-    def slot_of(home, d):
-        return (N - 1 + turn(home) * (d - home)) % N
-
-    order = sorted(range(N), key=lambda d: slot_of(r, d))
-    far, near = order[:2], order[2]
-    assert near == near_of(r) and order[3] == r
-    far_eng = topo.engines(core, cores[far[0]])
+    near = [d for d in range(N) if d != r and topo.chip(cores[d]) == topo.chip(core)][0]
+    others = [d for d in range(N) if topo.chip(cores[d]) != topo.chip(core)]
+    far1 = [d for d in others if topo.die(cores[d]) != topo.die(core)][0]
+    far2 = [d for d in others if d != far1][0]
+    order = [r, far1, far2, near]
+    far_eng = topo.engines(core, cores[far1])
     near_eng = [e for e in topo.engines(core, cores[near]) if e not in far_eng]
-    half = len(far_eng) // 2
-
-    def mask_of(es):
-        m = 0
-        for e in es:
-            m |= 1 << e
-        return m
-
-    far_masks = [mask_of(far_eng[:half]), mask_of(far_eng[half:])]
-    near_mask = mask_of(near_eng)
+    far_eng = far_eng[::len(far_eng) // CFG["far"]]
     sent = [0]
 
     def b8(ap):
         return ap.bitcast(dt.uint8)
 
-    def send_far(srcs, dsts, sem):
-        trs = []
-        for i, d in enumerate(far):
+    def send(trs, sem):
+        out = []
+        for d, es, src, dst in trs:
             rid, pid, _se = topo.addr(cores[d])
-            trs.append(RemoteDMATransfer(dst_ids=[DstId(rid=rid, pnc=pid)], dma_engine_mask=far_masks[i],
-                                         remote_sem=sem, src=srcs[i], dst=dsts[i]))
-        g.remote_dma_fused(trs, local_sem=T.sem.sent)
-        sent[0] += 2 * half
+            m = 0
+            for e in es:
+                m |= 1 << e
+            out.append(RemoteDMATransfer(dst_ids=[DstId(rid=rid, pnc=pid)], dma_engine_mask=m, remote_sem=sem,
+                                         src=src, dst=dst))
+            sent[0] += len(es)
+        g.remote_dma_fused(out, local_sem=T.sem.sent)
 
-    def send_near(src, dst, sem):
-        rid, pid, _se = topo.addr(cores[near])
-        g.remote_dma(dst, src, sem, T.sem.sent, pid, rid, near_mask)
-        sent[0] += len(near_eng)
+    def wave(items, sq, sp, dq, dp, sem):
+        send([(d, es, b8(sq[:, a:a + C]), b8(dq[:, z:z + C])) for d, es, a, z in items], sem)
+        send([(d, es, sp[:, a:a + C], dp[:, z:z + C]) for d, es, a, z in items], sem)
+        return 2 * sum(len(es) for d, es, a, z in items)
 
     def bank(b, n, c0=0):
         return T.pp[:, 512 * b + c0:512 * b + n]
@@ -124,20 +115,28 @@ def rank_program(g, core, T, topo):
     def fill(dst, n, value, t=None):
         return done(S.activation(dst, T.ones[:, 0:n], ACT.Identity, scale=value), t)
 
+    OWN, F1, F2, NR = [PAD + C * s for s in range(N)]
+
     runs = ((0, HW), (HW, TC))
     t_u = done(SY.dma_start(T.us[:], T.u[:]), k=16)
     t_x = [done(SY.dma_start(T.xs[:, 4 * j0:4 * j1], T.x[:, 4 * j0:4 * j1]), k=16) for j0, j1 in runs]
     t_a = done(SY.dma_start(b8(T.aq[:]), T.ac[:]), k=16)
     done(SY.dma_start(T.asc[:], T.ap[:]), t_a, 16)
-    t_c = done(SY.dma_start(b8(T.cq[:]), T.cc[:]), k=16)
-    done(SY.dma_start(T.csc[:], T.cp[:]), t_c, 16)
-    SY.wait_ge(T.sem.arr_far, 4 * half)
+    early = 1024 - 128 * CFG["late"]
+    t_c = done(SY.dma_start(T.csc[:], T.cp[:]), k=16)
+    done(SY.dma_start(b8(T.cq[:, 0:early]), T.cc[:, 0:4 * early]), t_c, 16)
+    t_go = tok()
+    wait_for("SY", t_go, 1)
+    t_c2 = t_c
+    if early < 1024:
+        t_c2 = done(SY.dma_start(b8(T.cq[:, early:1024]), T.cc[:, 4 * early:4096]), k=16)
     t_v = done(SY.dma_start(T.vs[:], T.v[:]), k=16)
 
     fl_ok = {"allow_small_or_imprecise_dtypes": True}
-    sg = turn(r)
+    sg = 1 if (r + 1) % N == order[1] else -1
+    assert [(r + sg * s) % N for s in range(N)] == order
     t_ip = done(g.iota(T.ip[:, 0:1], [[0, 1]], 0, 1))
-    done(g.iota(T.ip[:, 1:2], [[0, 1]], 4 * ((N - 1 - sg * r) % N) + 128, sg), t_ip)
+    done(g.iota(T.ip[:, 1:2], [[0, 1]], 4 * ((-sg * r) % N) + 128, sg), t_ip)
     t_ip2 = done(g.iota(T.ip[:, 2:3], [[0, 1]], 0, 17))
     t_ul = done(g.iota(T.ul[:], [[16, 8]], 0, 0))
     t_c152 = done(g.iota(T.c152[:], [[0, 38], [int(BIG), 4]], 0, 0, **fl_ok))
@@ -146,7 +145,7 @@ def rank_program(g, core, T, topo):
 
     t_ones = done(V.memset(T.ones[:], 1.0))
     wait("V", t_ones)
-    t_pad = done(V.tensor_copy(T.rr[:], T.ones[:]))
+    t_pad = done(V.tensor_copy(T.rr[:], T.ones[:, 0:320]))
     wait("V", t_ip)
     t_l1 = done(V.tensor_scalar(T.ci[:, 0:2], T.ip[:, 0:2], 2, 3, OP.logical_shift_right, OP.bitwise_and))
     done(V.tensor_scalar(T.ci[:, 2:3], T.ip[:, 0:1], 3, None, OP.bitwise_and), t_l1)
@@ -163,6 +162,11 @@ def rank_program(g, core, T, topo):
     wait("S", t_ones)
     t_z = fill(T.fl[:], TC, 0.0)
     t_win = fill(T.win[:, 0:4 * C], 4 * C, 4.0)
+
+    wait("G", t_ones)
+    t_e = tok()
+    for b in range(4):
+        done(g.affine_select(T.ebf[:, 512 * b:512 * b + 512], T.ones[:], [[1, 512]], OP.is_equal, 0.0, -b, -4), t_e)
 
     wait("V", t_u)
     t_qu = done(V.quantize_mx(T.uq[:], T.usc[:], T.us[:]))
@@ -187,24 +191,24 @@ def rank_program(g, core, T, topo):
     wait("S", t_s2, t_c152)
     t_g1 = done(S.activation(g1, qcol, ACT.Identity, scale=4.0, bias=g0))
     done(S.activation(T.csel[:], T.c152[:, 0:C], ACT.Relu, bias=nega), t_s3)
-    t_ez = tok()
-    for c0 in range(0, 2048, 256):
-        fill(T.ebf[:, c0:c0 + 256], 256, 0.0, t_ez)
-    wait("G", t_ones, t_ez)
-    t_e = tok()
-    for b in range(4):
-        done(g.affine_select(T.ebf[:, 512 * b + b:512 * b + 512:4], T.ones[:, 0:128], [[1, 128]], OP.is_equal, 0.0,
-                             0, -1), t_e)
-    t_hp = fill(T.hn[:, 0:4 * PAD], 4 * PAD, 0.0)
-    t_d = fill(T.d0[:, 0:64:2], 32, BIG)
+    t_hp = fill(T.xb[:, 0:512], 512, 0.0)
+    for i in range(2):
+        fill(T.hb[:, 4 * LW * i:4 * (LW * i + PAD)], 4 * PAD, 0.0, t_hp)
+    fill(T.zb[:, 0:4 * PAD], 4 * PAD, 0.0, t_hp)
+    t_d = fill(T.d0[:, 0:96:3], 32, HUGE)
+    fill(T.d1[:, 1:96:3], 32, HUGE, t_d)
     wait("S", t_jr)
-    done(S.activation(T.d1[:, 1:64:2], T.jr[:], ACT.Identity, bias=qcol), t_d)
+    done(S.activation(T.d1[:, 2:96:3], T.jr[:], ACT.Identity, bias=qcol), t_d)
     t_xw = tok()
     for b in RAW:
         fill(T.dw[:, DW * b + 4 * C:DW * (b + 1)], TC, 0.0, t_xw)
-    wait("S", *t_x)
+    wait("S", t_vals, *t_x)
     for b in SUM:
         done(S.activation(T.dw[:, DW * b + 4 * C:DW * (b + 1)], T.xs[:, b:4 * TC:4], ACT.Copy), t_xw)
+    t_tab = fill(T.tab[:, 4 * C:DW], TC, -1.0)
+    for s, d in enumerate(order):
+        done(S.activation(T.tab[:, C * s:C * s + C], T.vals[:, 0:C], ACT.Identity, scale=-0.25,
+                          bias=float(TC + C * d)), t_tab)
 
     tv = tok()
     for n, (j0, j1) in enumerate(runs):
@@ -240,8 +244,11 @@ def rank_program(g, core, T, topo):
     done(V.tensor_copy(T.win[:].indirect(T.loff[:, 0:NL]), T.vals[:]), tv)
 
     wait("S", t8, t_gl)
-    done(S.activation(T.d1[:, 0:64:2], places, ACT.Identity, scale=4.0, bias=-4.0), t_d)
-    done(S.activation(T.d0[:, 1:64:2], places, ACT.Relu, scale=4.0 * BIG, bias=-(4.0 * C + 3.5) * BIG), t_d)
+    t_rb = done(S.activation(T.rb[:], places, ACT.Identity, bias=127.625))
+    done(S.activation(T.d1[:, 0:96:3], places, ACT.Identity, scale=4.0 * C), t_d)
+    done(S.activation(T.d0[:, 2:96:3], places, ACT.Relu, scale=16.0 * BIG, bias=-(16.0 * C + 14.0) * BIG), t_d)
+    wait("S", t_rb)
+    done(S.activation(T.d0[:, 1:96:3], T.rb[:], ACT.Identity, scale=1.0 - 4 * C, bias=128.0 * (4 * C - 1) - 1), t_d)
 
     wait("V", tv, t_s3)
 
@@ -249,8 +256,8 @@ def rank_program(g, core, T, topo):
         return done(V.tensor_tensor_scan(T.sel[:, C * i:C * i + C], T.csel[:], T.win[:, i:4 * C:4], 0.0,
                                          OP.min, OP.max), t)
 
-    def offsets(lo):
-        return done(V.tensor_scalar(T.goff[:, 20 * lo:20 * lo + 40], T.sel[:, C * lo + 3:C * lo + HW:4], -1.0, top,
+    def offsets(lo, hi):
+        return done(V.tensor_scalar(T.goff[:, 20 * lo:20 * hi], T.sel[:, C * lo + 3:C * hi:4], -1.0, top,
                                     OP.mult, OP.add))
 
     def gather(q, dst, src, t=None):
@@ -259,235 +266,240 @@ def rank_program(g, core, T, topo):
         return done(S.activation(dst, src, ACT.Copy), t)
 
     def bundle(q, c0, c1, t=None):
-        return gather(q, T.xb[:, 16 * c0:16 * c1], T.xs[:].indirect(T.goff[:, c0:c1]), t)
+        return gather(q, T.xb[:, 4 * PAD + 16 * c0:4 * PAD + 16 * c1], T.xs[:].indirect(T.goff[:, c0:c1]), t)
 
-    select(0, tv)
-    select(1, tv)
-    t_s23 = select(2)
-    wait("V", tv)
-    t_ga = offsets(0)
-    select(3, t_s23)
-    wait("V", t_ga)
-    t_b01 = bundle("V", 0, 18)
-    wait("S", t_ga)
-    bundle("S", 18, 40, t_b01)
-    wait("V", t_s23)
-    t_gb = offsets(2)
-    wait("V", t_b01)
-    t_q1 = done(V.quantize_mx(T.qa[:], T.sa[:], T.xb[:, 0:4 * HW]))
-    wait("S", t_gb)
-    t_b23 = bundle("S", 40, 64)
-    wait("V", t_gb)
-    bundle("V", 64, 80, t_b23)
-    wait("V", t_b23)
-    t_q2 = done(V.quantize_mx(T.qb[:, 0:HW], T.sb[:, 0:HW], T.xb[:, 4 * HW:8 * HW]))
+    def pack(q, s, c0, src, s0, n, t=None):
+        return done(V.quantize_mx(q[:, c0:c0 + n], s[:, c0:c0 + n], src[:, 4 * s0:4 * (s0 + n)]), t)
 
-    at = [C * slot_of(d, r) for d in far]
+    t_sa = select(1)
+    t_sb = select(2)
+    wait("V", t_sa)
+    t_oa = offsets(1, 2)
+    select(3, t_sb)
+    wait("V", t_oa)
+    t_ba = bundle("V", 20, 20 + CFG["g0"])
+    wait("S", t_oa)
+    bundle("S", 20 + CFG["g0"], 40, t_ba)
+    wait("V", t_sb)
+    t_ob = offsets(2, 4)
+    wait("V", t_ba, t_hp)
+    t_q1 = pack(T.oq, T.op, 0, T.xb, F1 - PAD, 128)
+    wait("V", t_ob)
+    t_bb = bundle("V", 40, 40 + CFG["g12"])
+    wait("S", t_ob)
+    bundle("S", 40 + CFG["g12"], 80, t_bb)
+    t_sc = select(0)
+    wait("V", t_sc)
+    t_oc = offsets(0, 1)
+    wait("V", t_bb)
+    t_q2 = pack(T.oq, T.op, 128, T.xb, F2, HW)
+    wait("S", t_oc, t_q1)
+    t_bc = bundle("S", CFG["g3"], 20)
+    wait("V", t_oc, t_q1)
+    bundle("V", 0, CFG["g3"], t_bc)
+    wait("V", t_bc)
+    t_q3 = pack(T.lq, T.lp, 0, T.xb, 0, 128)
+
+    out_eng = near_eng[::len(near_eng) // CFG["near"]]
+    home_eng = near_eng[::len(near_eng) // CFG["nearh"]]
     wait("G", t_q1)
-    send_far([b8(T.qa[:, C * i:C * i + C]) for i in range(2)], [b8(T.la[:, a:a + C]) for a in at], T.sem.arr_far)
-    send_far([T.sa[:, C * i:C * i + C] for i in range(2)], [T.las[:, a:a + C] for a in at], T.sem.arr_far)
+    n_out1 = wave([(far1, far_eng, PAD, F1)], T.oq, T.op, T.lq, T.lp, T.sem.out1)
     wait("G", t_q2)
-    send_near(b8(T.qb[:, 0:C]), b8(T.qb[:, HW:HW + C]), T.sem.arr_near)
-    send_near(T.sb[:, 0:C], T.sb[:, HW:HW + C], T.sem.arr_near)
+    n_out2 = wave([(far2, far_eng, 128, F2), (near, out_eng, 128 + C, NR)], T.oq, T.op, T.lq, T.lp, T.sem.out2)
+    g.sem_inc(t_go["sem"], 1)
+    t_go["n"] += 1
 
-    t_tab = tok()
-    for s, d in enumerate(order):
-        done(g.iota(T.tab[:, s:4 * C:4], [[1, C]], C * d, 0, **fl_ok), t_tab)
-    done(g.iota(T.tab[:, 4 * C:DW], [[0, TC]], -1, 0, **fl_ok), t_tab)
+    one, two = (lambda c: (c - PAD, 128, PAD)), (lambda c: (c, HW, 0))
+    passes = {"o": one(OWN), "F": one(F1), "W": two(F2), "1": one(F1), "2": two(F2)}
+    banks = {"oA0": 4, "oA1": 0, "FA0": 4, "FA1": 0, "WA0": 4, "WA1": 0, "1C": 4, "2C": 0, "oC": 4}
+    before = {"oA1": None, "oA0": None, "FA0": "o0", "FA1": "o1", "WA0": "F0", "WA1": "F1", "1C": "W0", "2C": "W1",
+              "oC": "12"}
+    made_in = {"o": "o", "1": "F", "2": "W"}
+    stage_of = {p + str(n): p + ("A%d" % n if n < 2 else "C") for p in "oFW12" for n in range(3)}
+    t_bank = [tok() for b in range(8)]
+    uses = {}
+    count = [0] * 8
+    for st in ["oA0", "oA1"] + CFG["pe"].split() + ["oC"]:
+        st = st[:2] if st[1] == "C" else st
+        if st not in uses:
+            for b in range(4):
+                count[banks[st] + b] += 1
+            uses[st] = count[banks[st]]
+    t_ev = {k: tok() for k in ("o0", "o1", "o2", "F0", "F1", "W0", "W1", "12", "22")}
+    t_q = {k: tok() for k in t_ev}
 
-    def relu(q, dst, src, t):
-        if q == "V":
-            return done(V.tensor_scalar(dst, src, 0.0, 0.0625, OP.max, OP.mult), t)
-        return done(S.activation(dst, src, ACT.Relu, scale=0.0625), t)
+    def z_col(c):
+        return c - C if c >= F1 else c + 3 * C
 
-    def scaled(q, dst, src, t):
-        if q == "V":
-            return done(V.tensor_scalar(dst, src, 0.0625, None, OP.mult), t)
-        return done(S.activation(dst, src, ACT.Identity, scale=0.0625), t)
-
-    def product(q, s, i, b, b0, m, start, stop):
+    def product(q, s, i, b, st, mq, ms, c0, start, stop):
         k = 512 * i + 128 * b
-        ins = PE.matmul_mx(bank(b0 + b, m[2]), q[:, k:k + 128], s[:, k:k + 128], m[0], m[1], start, stop)
-        return done(ins) if stop else None
+        m0, n, _f = passes[st[0]]
+        ins = PE.matmul_mx(bank(banks[st] + b, n), q[:, k:k + 128], s[:, k:k + 128], mq[:, c0 + m0:c0 + m0 + n],
+                           ms[:, c0 + m0:c0 + m0 + n], start, stop)
+        if stop:
+            done(ins, t_bank[banks[st] + b])
 
-    def layer_a(i, b0, m):
-        return [product(T.aq, T.asc, i, b, b0, m, True, True) for b in range(4)]
+    def layer(st):
+        key = st[:2] if st[1] == "C" else st
+        if before[key] is not None:
+            wait_for("PE", t_ev[before[key]], 4)
+        if st[1] == "A":
+            for b in range(4):
+                product(T.aq, T.asc, int(st[2]), b, st, T.lq, T.lp, 0, True, True)
+            return
+        steps = [(int(st[2]), b) for b in range(4)] if len(st) == 3 else [(i, b) for b in range(4) for i in range(2)]
+        for i, b in steps:
+            wait_for("PE", t_q[made_in[st[0]] + str(i)], 1)
+            wait("PE", t_c if 512 * i + 128 * b < early else t_c2)
+            product(T.cq, T.csc, i, b, key, T.hq, T.hp, LW * i, i == 0, i == 1)
 
-    def layer_c(i, b0, m):
-        return [product(T.cq, T.csc, i, b, b0, m, i == 0, i == 1) for b in range(4)]
-
-    def width(p):
-        return HW if p == "f" else 128
-
-    def tile_out(p, n, b):
-        if p == "f":
-            return T.hf[:, 4 * HW * n + b:4 * HW * (n + 1):4]
-        c0 = PAD + C * (n + (3 if p == "n" else 0))
-        return T.hn[:, 4 * c0 + b:4 * (c0 + C):4]
-
-    def tile_in(p, n):
-        if p == "f":
-            return T.hf[:, 4 * HW * n:4 * HW * (n + 1)]
-        c0 = C * (n + (3 if p == "n" else 0))
-        return T.hn[:, 4 * c0:4 * (c0 + 128)]
-
-    def packed(p, n):
-        w = width(p)
-        if n < 2:
-            c0 = {"f": HW * n, "o": 2 * HW + 128 * n, "n": 2 * HW + 256 + 128 * n}[p]
-            return T.hq[:, c0:c0 + w], T.hs[:, c0:c0 + w], w
-        c0 = {"f": 0, "o": HW, "n": HW + 128}[p]
-        return T.zq[:, c0:c0 + w], T.zs[:, c0:c0 + w], w
-
-    ev_tok = {}
-
-    def evict(q, p, n, b0, ts, bs):
-        t = ev_tok.setdefault((p, n), None) or tok()
-        ev_tok[p, n] = t
+    def evict(q, k, bs):
+        st, n = stage_of[k], int(k[1])
+        m0, w, f = passes[k[0]]
         for b in bs:
-            wait(q, ts[b])
-            (relu if n < 2 else scaled)(q, tile_out(p, n, b), bank(b0 + b, width(p), 0 if p == "f" else PAD), t)
-        return t
+            wait_for(q, t_bank[banks[st] + b], uses[st])
+            src = bank(banks[st] + b, w, f)
+            if n < 2:
+                c = LW * n + m0 + f
+                dst = T.hb[:, 4 * c + b:4 * (c + w - f):4]
+                ins = (V.tensor_scalar(dst, src, 0.0, 0.0625, OP.max, OP.mult) if q == "V" else
+                       S.activation(dst, src, ACT.Relu, scale=0.0625))
+            else:
+                c = z_col(m0 + f)
+                dst = T.zb[:, 4 * c + b:4 * (c + w - f):4]
+                ins = (V.tensor_scalar(dst, src, 0.0625, None, OP.mult) if q == "V" else
+                       S.activation(dst, src, ACT.Identity, scale=0.0625))
+            done(ins, t_ev[k])
 
-    def quantise(p, n):
-        wait("V", ev_tok[p, n])
-        q, s, _w = packed(p, n)
-        return done(V.quantize_mx(q, s, tile_in(p, n)))
+    def quantise(k):
+        n = int(k[1])
+        m0, w, f = passes[k[0]]
+        wait_for("V", t_ev[k], 4)
+        if n < 2:
+            pack(T.hq, T.hp, LW * n + m0, T.hb, LW * n + m0, w, t_q[k])
+        elif k[0] == "o":
+            pack(T.zl, T.zlp, 0, T.zb, LW - 128, 128, t_q[k])
+        else:
+            pack(T.zq, T.zp, HW * (int(k[0]) - 1), T.zb, z_col(m0 + f) - f, w, t_q[k])
 
-    def quantise_e(b0, b1, t=None):
-        return done(V.quantize_mx(T.eq[:, 128 * b0:128 * b1], T.esc[:, 128 * b0:128 * b1],
-                                  T.ebf[:, 512 * b0:512 * b1]), t)
+    t_qe = tok()
 
-    mo = (T.qb[:, HW - 128:HW], T.sb[:, HW - 128:HW], 128)
-    wait("PE", tv, t_a, t_q2)
-    o0 = layer_a(0, 0, mo)
-    o1 = layer_a(1, 4, mo)
+    def follow(q, steps):
+        for w in steps.split():
+            if w[0] == "e":
+                evict(q, w[1:3], [int(b) for b in w[4:]])
+            elif w[0] == "q":
+                quantise(w[1:3])
+            else:
+                b0, b1 = int(w[1]), int(w[2])
+                wait("V", t_e)
+                pack(T.eq, T.esc, 128 * b0, T.ebf, 128 * b0, 128 * (b1 - b0), t_qe)
+
+    wait("PE", tv, t_a, t_q3)
+    layer("oA0")
+    layer("oA1")
     wait("V", t_d)
-    done(V.tensor_tensor_scan(T.d2[:], T.d0[:], T.d1[:], 0.0, OP.add, OP.min), tv)
-    evict("S", "o", 0, 0, o0, (0, 1, 2))
-    evict("V", "o", 0, 0, o0, (3,))
+    done(V.tensor_tensor_scan(T.d2[:], T.d0[:, 0:3 * NL], T.d1[:, 0:3 * NL], 0.0, OP.add, OP.min), tv)
+    evict("S", "o0", (0, 1, 2))
+    evict("V", "o0", (3,))
     wait("V", tv)
-    t_h = done(V.tensor_copy(T.hoff[:], T.d2[:, 1:2 * NL:2]))
-    wait("V", t_hp)
-    q_o0 = quantise("o", 0)
-    evict("S", "o", 1, 4, o1, (0, 1, 2))
-    evict("V", "o", 1, 4, o1, (3,))
-    q_o1 = quantise("o", 1)
-    wait("V", t_e)
-    t_qe = quantise_e(0, 2)
-    wait("PE", t_c, q_o0)
-    layer_c(0, 0, packed("o", 0))
-    wait("PE", q_o1)
-    oc_ = layer_c(1, 0, packed("o", 1))
-    evict("S", "o", 2, 0, oc_, (0, 1, 2))
-    evict("V", "o", 2, 0, oc_, (3,))
-    q_oz = quantise("o", 2)
-    quantise_e(2, 4, t_qe)
+    t_h = done(V.tensor_copy(T.hoff[:], T.d2[:, 2:3 * NL:3]))
+    quantise("o0")
+    evict("S", "o1", (0, 1, 2))
+    evict("V", "o1", (3,))
+    quantise("o1")
+    wait("V", t_q["o0"], t_q["o1"])
 
-    mf = (T.la[:], T.las[:], HW)
-    mn = (T.qb[:, 3 * C - 128:3 * C], T.sb[:, 3 * C - 128:3 * C], 128)
-    PE.wait_ge(T.sem.arr_far, 4 * half)
-    f0 = layer_a(0, 4, mf)
-    wait("PE", ev_tok["o", 2])
-    f1 = layer_a(1, 0, mf)
-    evict("V", "f", 0, 4, f0, (0, 2))
-    evict("S", "f", 0, 4, f0, (1, 3))
-    q_f0 = quantise("f", 0)
-    evict("S", "f", 1, 0, f1, (0, 1, 3))
-    evict("V", "f", 1, 0, f1, (2,))
-    q_f1 = quantise("f", 1)
-    wait("PE", ev_tok["f", 0])
-    PE.wait_ge(T.sem.arr_near, 2 * len(near_eng))
-    n0 = layer_a(0, 4, mn)
-    wait("PE", q_f0, ev_tok["f", 1])
-    layer_c(0, 0, packed("f", 0))
-    wait("PE", q_f1)
-    fc = layer_c(1, 0, packed("f", 1))
-    evict("S", "n", 0, 4, n0, (0, 1, 2, 3))
-    wait("PE", ev_tok["n", 0])
-    n1 = layer_a(1, 4, mn)
-    q_n0 = quantise("n", 0)
-    evict("V", "f", 2, 0, fc, (0, 2))
-    evict("S", "f", 2, 0, fc, (1, 3))
-    q_fz = quantise("f", 2)
-    evict("S", "n", 1, 4, n1, (0, 1, 2))
-    evict("V", "n", 1, 4, n1, (3,))
-    q_n1 = quantise("n", 1)
-    wait("PE", q_n0, ev_tok["f", 2])
-    layer_c(0, 0, packed("n", 0))
-    wait("PE", q_n1)
-    nc = layer_c(1, 0, packed("n", 1))
-    evict("V", "n", 2, 0, nc, (0, 2))
-    evict("S", "n", 2, 0, nc, (1, 3))
-    q_nz = quantise("n", 2)
+    for st in CFG["pe"].split():
+        if st == "FA0":
+            PE.wait_ge(T.sem.out1, n_out1)
+        if st == "WA0":
+            PE.wait_ge(T.sem.out2, n_out2)
+        layer(st)
+    follow("V", CFG["v"])
+    follow("S", CFG["s"])
 
-    wait("G", q_fz)
-    send_far([b8(T.zq[:, C * a:C * a + C]) for a in range(2)], [b8(T.zl[:, a:a + C]) for a in at], T.sem.home_far)
-    send_far([T.zs[:, C * a:C * a + C] for a in range(2)], [T.zls[:, a:a + C] for a in at], T.sem.home_far)
-    zn = HW + 128 + PAD
-    wait("G", q_nz)
-    send_near(b8(T.zq[:, zn:zn + C]), b8(T.zl[:, HW:HW + C]), T.sem.home_near)
-    send_near(T.zs[:, zn:zn + C], T.zls[:, HW:HW + C], T.sem.home_near)
+    wait("G", t_q["12"])
+    n_home1 = wave([(far1, far_eng, PAD, F1)], T.zq, T.zp, T.zl, T.zlp, T.sem.home1)
+    wait("G", t_q["22"])
+    n_home2 = wave([(far2, far_eng, HW, F2), (near, home_eng, HW + C, NR)], T.zq, T.zp, T.zl, T.zlp, T.sem.home2)
 
-    def decode(b0, m, slots, ts):
-        for b in range(4):
-            t = done(PE.matmul_mx(bank(b0 + b, m[2]), T.eq[:, 128 * b:128 * b + 128],
-                                  T.esc[:, 128 * b:128 * b + 128], m[0], m[1], True, True))
-            for k, s in enumerate(slots):
-                c0 = m[2] - C * (len(slots) - k)
-                dst, src = T.dw[:, DW * b + s:DW * b + 4 * C:4], bank(b0 + b, c0 + C, c0)
-                if b in RAW:
-                    wait("S", t)
-                    done(S.activation(dst, src, ACT.Copy), ts[b])
-                else:
-                    wait("V", t)
-                    done(V.tensor_tensor(dst, src, T.xb[:, 4 * C * s + b:4 * C * (s + 1):4], OP.add), ts[b])
-
-    t_own, t_far = tok(), tok()
-    wait("PE", t_qe, q_oz, ev_tok["n", 1])
-    decode(4, packed("o", 2), (3,), [t_own] * 4)
-    wait("V", t_v)
-    t_qv = done(V.quantize_mx(T.vq[:], T.vsc[:], T.vs[:]))
+    layer("oC")
+    follow("S", CFG["so"])
+    follow("V", CFG["vo"])
     wait("S", t_h, t_tab)
     t_olr = done(S.activation(T.olr[:], T.tab[:].indirect(T.hoff[:]), ACT.Copy))
     wait("SY", t_olr)
     t_out = done(SY.dma_start(T.ol[:], T.olr[0:128:16, :]), k=16)
 
-    wait("PE", ev_tok["n", 2])
-    PE.wait_ge(T.sem.home_far, 4 * half)
-    decode(0, (T.zl[:, 0:HW], T.zls[:, 0:HW], HW), (0, 1), [t_far] * 4)
-    wait("PE", t_own)
-    PE.wait_ge(T.sem.home_near, 2 * len(near_eng))
+    def decode(b0, s, ts):
+        m0 = PAD + C * s
+        for b in CFG["dec"]:
+            t = done(PE.matmul_mx(bank(b0 + b, HW), T.eq[:, 128 * b:128 * b + 128], T.esc[:, 128 * b:128 * b + 128],
+                                  T.zl[:, m0:m0 + HW], T.zlp[:, m0:m0 + HW], True, True), t_bank[b0 + b])
+            dst, src = T.dw[:, DW * b + C * s:DW * b + C * s + HW], bank(b0 + b, HW)
+            if b in RAW:
+                wait("S", t)
+                done(S.activation(dst, src, ACT.Copy), ts[b])
+            else:
+                wait("V", t)
+                done(V.tensor_tensor(dst, src, T.xb[:, 4 * m0 + b:4 * (m0 + HW):4], OP.add), ts[b])
+
+    t_first = tok()
+    wait("V", t_v)
+    t_qv = done(V.quantize_mx(T.vq[:], T.vsc[:], T.vs[:]))
     t_dn = [tok() for b in range(4)]
-    decode(4, (T.zl[:, 3 * C - 128:3 * C], T.zls[:, 3 * C - 128:3 * C], 128), (2,), t_dn)
-    wait("V", t_h, t_own, t_far, t_xw)
-    wait("S", t_own, t_far, t_xw)
-    wait("PE", t_far, t_qv)
+    wait("PE", t_qe, t_q["o2"], t_ev["22"])
+    PE.wait_ge(T.sem.home1, n_home1)
+    decode(0, 0, [t_first] * 4)
+    wait("PE", t_ev["o2"])
+    PE.wait_ge(T.sem.home2, n_home2)
+    decode(4, 2, t_dn)
+    wait("V", t_h, t_first, t_xw)
+    wait("S", t_h, t_first, t_xw)
+    wait("PE", t_first, t_qv)
 
     ty = [tok(), tok()]
 
-    def pick_y(n, b):
-        j0, j1 = runs[n]
-        dst = T.yb[:, 4 * j0 + b:4 * j1:4]
-        src = T.dw[:, DW * b:DW * (b + 1)].indirect(T.hoff[:, j0 // 16:j1 // 16])
+    def pick_y(q, n, b, c0, c1):
+        dst = T.yb[:, 64 * c0 + b:64 * c1:4]
+        src = T.dw[:, DW * b:DW * (b + 1)].indirect(T.hoff[:, c0:c1])
+        wait(q, t_dn[b])
         if b in RAW:
-            wait("V", t_dn[b])
-            done(V.tensor_tensor(dst, src, T.xs[:, 4 * j0 + b:4 * j1:4], OP.add), ty[n])
+            done(V.tensor_tensor(dst, src, T.xs[:, 64 * c0 + b:64 * c1:4], OP.add), ty[n])
         else:
-            wait("S", t_dn[b])
-            gather("S", dst, src, ty[n])
+            gather(q, dst, src, ty[n])
+
+    def shares(n):
+        c0, c1 = runs[n][0] // 16, runs[n][1] // 16
+        out = [("V", b, c0, c1) for b in RAW]
+        for b in [b for b in CFG["dec"] if b in SUM]:
+            mine = [(a, z) for bb, a, z in CFG["yv"] if bb == b and c0 <= a < c1]
+            if not mine:
+                out.append(("S", b, c0, c1))
+                continue
+            a, z = mine[0]
+            out.append(("V", b, a, z))
+            if a > c0:
+                out.append(("S", b, c0, a))
+            if z < c1:
+                out.append(("S", b, z, c1))
+        return out
 
     for n in range(2):
-        for b in SUM:
-            pick_y(n, b)
+        for q, b, c0, c1 in shares(n):
+            if q == "S":
+                pick_y(q, n, b, c0, c1)
     tq, tm = [None, None], [None, None]
     for n, (j0, j1) in enumerate(runs):
-        for b in RAW:
-            pick_y(n, b)
+        for q, b, c0, c1 in shares(n):
+            if q == "V":
+                pick_y(q, n, b, c0, c1)
         wait("V", ty[n])
-        tq[n] = done(V.quantize_mx(T.yq[:, j0:j1], T.ysc[:, j0:j1], T.yb[:, 4 * j0:4 * j1]))
+        tq[n] = pack(T.yq, T.ysc, j0, T.yb, j0, j1 - j0)
         wait("PE", tq[n])
-        tm[n] = done(PE.matmul_mx(bank(n, j1 - j0), T.vq[:], T.vsc[:], T.yq[:, j0:j1], T.ysc[:, j0:j1], True, True))
+        tm[n] = done(PE.matmul_mx(bank(n, j1 - j0), T.vq[:], T.vsc[:], T.yq[:, j0:j1], T.ysc[:, j0:j1],
+                                  True, True), t_bank[n])
         wait("SY", tq[n])
         done(SY.dma_start(T.oc[:, 4 * j0:4 * j1], b8(T.yq[:, j0:j1])), t_out, 16)
     wait("S", tm[0])

@@ -1,20 +1,27 @@
 from concourse.bass import DstId, RemoteDMATransfer
 from concourse.mybir import dt, AluOpType, ActivationFunctionType
 
-CFG = {"near": 4, "nearh": 4, "far": 8, "late": 3, "raw": (0,), "g0": 10, "g12": 16, "g3": 8, "pe": "FA0 FA1 WA0 WA1 1C 2C0 2C1", "v": "eF0:13 qF0 eF1:3 qF1 eW0:13 qW0 eW1:3 qW1 e12:3 q12 E02 e22:13 q22", "s": "eF0:02 eF1:012 eW0:02 eW1:012 e12:012 e22:02", "dec": (1, 0, 2, 3), "yv": ((3, 0, 6), (3, 10, 12)), "vo": "E24 eo2:3 qo2", "so": "eo2:012"}
-
 N, TC, C = 4, 288, 80
 HW = 2 * C
 PAD = 128 - C
 LW = PAD + 4 * C
 DW = 4 * C + TC
+K = 512
 BIG = 2048.0
 HUGE = 512 * BIG
+WHOLE = 192.0
 NL = TC // 16
+EW = 528
+EARLY = 640
 Q4, U8, BF, F32, I32, U16 = "float8_e4m3fn_x4", "uint8", "bfloat16", "float32", "int32", "uint16"
 F16 = "float16"
-RAW = CFG["raw"]
-SUM = tuple(b for b in range(4) if b not in RAW)
+RAW = 0
+UNPACK = (1, 0, 2, 3)
+
+ON_TENSOR = "oA0 oA1 FA0 FA1 WA0 WA1 1C 2C0 2C1 oC"
+ON_VECTOR = ("eo0:13 eo1:13 eF0:13 qF0 eF1:3 eW0:1 qF1 eW0:3 qW0 eW1:3 qW1 e12:3 q12 E0 e22:13 q22 E123 "
+             "eo2:3 qo2")
+ON_SCALAR = "eo0:02 eo1:02 eF0:02 eF1:012 eW0:02 eW1:012 e12:012 e22:02 eo2:012"
 
 
 def _sb(n, d):
@@ -27,18 +34,18 @@ SCRATCH = {
     "xq": _sb(TC, Q4), "xsc": _sb(TC, U8),
     "uq": _sb(128, Q4), "usc": _sb(128, U8), "uq2": _sb(128, Q4), "usc2": _sb(128, U8),
     "vq": _sb(128, Q4), "vsc": _sb(128, U8),
-    "ones": _sb(512, BF), "ebf": _sb(2048, BF), "eq": _sb(512, Q4), "esc": _sb(512, U8),
-    "ip": _sb(3, I32), "ci": _sb(5, I32), "cf": _sb(5, F32), "cs": _sb(5, F32), "ul": _sb(8, I32),
+    "ones": _sb(514, BF), "ebf": _sb(2 * EW, BF), "eq": _sb(512, Q4), "esc": _sb(512, U8),
+    "ip": _sb(2, I32), "ci": _sb(4, I32), "cf": _sb(4, F32), "cs": _sb(5, F32), "ul": _sb(8, I32),
     "uoff": _sb(8, U16), "gl": _sb(2, U16),
-    "csel": _sb(C, F32), "c152": _sb(152, F32), "vals": _sb(TC, F32),
-    "pt": _sb(TC, F32), "mm": _sb(36, F32), "ww": _sb(36, F32), "ff": _sb(36, F32),
-    "fl": _sb(TC, BF), "fr": _sb(TC, BF), "cum": _sb(TC, F16), "rr": _sb(320, F16), "tt": _sb(608, F16),
-    "s152": _sb(152, F32), "loff": _sb(32, U16), "win": _sb(4 * TC, F32), "sel": _sb(4 * C, F32),
+    "csel": _sb(C, F32), "c80": _sb(C, F32), "vals": _sb(TC, F32),
+    "pt": _sb(TC, F32), "mm": _sb(36, F32), "ww": _sb(36, F32), "wn": _sb(36, F32), "ff": _sb(36, F32),
+    "nf": _sb(608, BF), "fr": _sb(320, BF), "rr": _sb(320, F16), "tt": _sb(608, F16),
+    "s152": _sb(152, F32), "loff": _sb(32, U16), "win": _sb(N * K, F32), "sel": _sb(4 * C, F32),
     "goff": _sb(C, U16), "xb": _sb(4 * LW, BF),
     "oq": _sb(128 + HW, Q4), "op": _sb(128 + HW, U8), "lq": _sb(LW, Q4), "lp": _sb(LW, U8),
-    "hb": _sb(8 * LW, BF), "hq": _sb(2 * LW, Q4), "hp": _sb(2 * LW, U8),
-    "zb": _sb(4 * LW, BF), "zq": _sb(2 * HW, Q4), "zp": _sb(2 * HW, U8), "zl": _sb(LW, Q4), "zlp": _sb(LW, U8),
-    "jr": _sb(32, F32), "d0": _sb(96, F32), "d1": _sb(96, F32), "d2": _sb(3 * NL, F32), "rb": _sb(32, BF),
+    "hb": _sb(16 * HW, BF), "hq": _sb(4 * HW, Q4), "hp": _sb(4 * HW, U8),
+    "zb": _sb(4 * LW, BF), "zq": _sb(128 + HW, Q4), "zp": _sb(128 + HW, U8), "zl": _sb(LW, Q4), "zlp": _sb(LW, U8),
+    "jr": _sb(32, F32), "d0": _sb(128, F32), "d1": _sb(128, F32), "d2": _sb(4 * NL, F32), "rb": _sb(96, BF),
     "hoff": _sb(NL, U16), "tab": _sb(DW, F32), "olr": _sb(TC, F32),
     "dw": _sb(4 * DW, BF), "yb": _sb(4 * TC, BF), "yq": _sb(TC, Q4), "ysc": _sb(TC, U8), "yo": _sb(TC, F32),
     "pp": ("psum", [128, 4096], F32),
@@ -85,8 +92,7 @@ def rank_program(g, core, T, topo):
     far2 = [d for d in others if d != far1][0]
     order = [r, far1, far2, near]
     far_eng = topo.engines(core, cores[far1])
-    near_eng = [e for e in topo.engines(core, cores[near]) if e not in far_eng]
-    far_eng = far_eng[::len(far_eng) // CFG["far"]]
+    near_eng = [e for e in topo.engines(core, cores[near]) if e not in far_eng][::2]
     sent = [0]
 
     def b8(ap):
@@ -107,7 +113,7 @@ def rank_program(g, core, T, topo):
     def wave(items, sq, sp, dq, dp, sem):
         send([(d, es, b8(sq[:, a:a + C]), b8(dq[:, z:z + C])) for d, es, a, z in items], sem)
         send([(d, es, sp[:, a:a + C], dp[:, z:z + C]) for d, es, a, z in items], sem)
-        return 2 * sum(len(es) for d, es, a, z in items)
+        return sem, 2 * sum(len(es) for d, es, a, z in items)
 
     def bank(b, n, c0=0):
         return T.pp[:, 512 * b + c0:512 * b + n]
@@ -122,57 +128,57 @@ def rank_program(g, core, T, topo):
     t_x = [done(SY.dma_start(T.xs[:, 4 * j0:4 * j1], T.x[:, 4 * j0:4 * j1]), k=16) for j0, j1 in runs]
     t_a = done(SY.dma_start(b8(T.aq[:]), T.ac[:]), k=16)
     done(SY.dma_start(T.asc[:], T.ap[:]), t_a, 16)
-    early = 1024 - 128 * CFG["late"]
     t_c = done(SY.dma_start(T.csc[:], T.cp[:]), k=16)
-    done(SY.dma_start(b8(T.cq[:, 0:early]), T.cc[:, 0:4 * early]), t_c, 16)
+    done(SY.dma_start(b8(T.cq[:, 0:EARLY]), T.cc[:, 0:4 * EARLY]), t_c, 16)
     t_go = tok()
     wait_for("SY", t_go, 1)
-    t_c2 = t_c
-    if early < 1024:
-        t_c2 = done(SY.dma_start(b8(T.cq[:, early:1024]), T.cc[:, 4 * early:4096]), k=16)
+    t_c2 = done(SY.dma_start(b8(T.cq[:, EARLY:1024]), T.cc[:, 4 * EARLY:4096]), k=16)
     t_v = done(SY.dma_start(T.vs[:], T.v[:]), k=16)
 
     fl_ok = {"allow_small_or_imprecise_dtypes": True}
-    sg = 1 if (r + 1) % N == order[1] else -1
-    assert [(r + sg * s) % N for s in range(N)] == order
     t_ip = done(g.iota(T.ip[:, 0:1], [[0, 1]], 0, 1))
-    done(g.iota(T.ip[:, 1:2], [[0, 1]], 4 * ((-sg * r) % N) + 128, sg), t_ip)
-    t_ip2 = done(g.iota(T.ip[:, 2:3], [[0, 1]], 0, 17))
     t_ul = done(g.iota(T.ul[:], [[16, 8]], 0, 0))
-    t_c152 = done(g.iota(T.c152[:], [[0, 38], [int(BIG), 4]], 0, 0, **fl_ok))
+    t_ip2 = done(g.iota(T.ip[:, 1:2], [[0, 1]], 0, 17))
+    t_c80 = done(g.iota(T.c80[:], [[0, C // 4], [int(BIG), 4]], 0, 0, **fl_ok))
     t_vals = done(g.iota(T.vals[:], [[-4, TC]], 4 * TC, 0, **fl_ok))
     t_jr = done(g.iota(T.jr[:], [[16, 32]], 4 * C, 0, **fl_ok))
 
+    acol, tcol, qcol, pcol = [T.cf[:, k:k + 1] for k in range(4)]
+    winit, nega, top, g0, g1 = [T.cs[:, k:k + 1] for k in range(5)]
     t_ones = done(V.memset(T.ones[:], 1.0))
+    wait("V", t_ip)
+    t_l0 = done(V.tensor_scalar(T.ci[:, 0:1], T.ip[:, 0:1], 2, 3, OP.logical_shift_right, OP.bitwise_and))
+    t_l1 = done(V.tensor_scalar(T.ci[:, 1:2], T.ip[:, 0:1], 3, None, OP.bitwise_and))
+    done(V.tensor_scalar(T.ci[:, 2:3], T.ip[:, 0:1], 15, None, OP.bitwise_and), t_l1)
+    wait("V", t_l0)
+    t_l2 = done(V.tensor_copy(T.cf[:, 0:1], T.ci[:, 0:1]))
+    wait("V", t_ip2)
+    done(V.tensor_scalar(T.ci[:, 3:4], T.ip[:, 1:2], 4, 1, OP.logical_shift_right, OP.bitwise_and), t_l1)
     wait("V", t_ones)
     t_pad = done(V.tensor_copy(T.rr[:], T.ones[:, 0:320]))
-    wait("V", t_ip)
-    t_l1 = done(V.tensor_scalar(T.ci[:, 0:2], T.ip[:, 0:2], 2, 3, OP.logical_shift_right, OP.bitwise_and))
-    done(V.tensor_scalar(T.ci[:, 2:3], T.ip[:, 0:1], 3, None, OP.bitwise_and), t_l1)
-    done(V.tensor_scalar(T.ci[:, 3:4], T.ip[:, 0:1], 15, None, OP.bitwise_and), t_l1)
-    wait("V", t_ip2)
-    done(V.tensor_scalar(T.ci[:, 4:5], T.ip[:, 2:3], 4, 1, OP.logical_shift_right, OP.bitwise_and), t_l1)
-    wait("V", t_l1)
-    t_l2 = done(V.tensor_copy(T.cf[:], T.ci[:]))
-    acol, wcol, tcol, qcol, pcol = [T.cf[:, k:k + 1] for k in range(5)]
-    winit, nega, top, g0, g1 = [T.cs[:, k:k + 1] for k in range(5)]
-    wait("V", t_l2, t_ul)
+    wait("V", t_ul, t_l2)
     t_uo = done(V.tensor_scalar(T.uoff[:], T.ul[:], acol, None, OP.add))
+    wait("V", t_l1)
+    done(V.tensor_copy(T.cf[:, 1:4], T.ci[:, 1:4]), t_l2)
+    done(V.tensor_copy(T.fr[:], T.ones[:, 0:320]), t_pad)
 
+    fl = T.nf[:, 320:608]
     wait("S", t_ones)
-    t_z = fill(T.fl[:], TC, 0.0)
-    t_win = fill(T.win[:, 0:4 * C], 4 * C, 4.0)
+    t_z = fill(fl, TC, 0.0)
+    t_win = tok()
+    for e in range(N):
+        fill(T.win[:, K * e:K * e + C], C, 4.0, t_win)
 
     wait("G", t_ones)
     t_e = tok()
-    for b in range(4):
-        done(g.affine_select(T.ebf[:, 512 * b:512 * b + 512], T.ones[:], [[1, 512]], OP.is_equal, 0.0, -b, -4), t_e)
+    for k in range(2):
+        done(g.affine_select(T.ebf[:, EW * k:EW * k + 514], T.ones[:], [[1, 514]], OP.is_equal, 0.0, -2 - k, -4), t_e)
 
     wait("V", t_u)
     t_qu = done(V.quantize_mx(T.uq[:], T.usc[:], T.us[:]))
-    wait("V", t_qu, t_uo)
+    wait("V", t_uo, t_qu)
     t_pu = done(V.tensor_copy(T.uq2[:].bitcast(dt.uint32), T.uq[:].bitcast(dt.uint32).indirect(T.uoff[:])))
-    wait("S", t_qu, t_uo)
+    wait("S", t_uo, t_qu)
     done(S.activation(T.usc2[:], T.usc[:].indirect(T.uoff[:]), ACT.Copy), t_pu)
     wait("PE", t_pu)
     t_p = []
@@ -184,31 +190,25 @@ def rank_program(g, core, T, topo):
                                      True, True)))
 
     wait("S", t_l2)
-    t_s1 = done(S.activation(winit, wcol, ACT.Identity, scale=0.25))
+    t_s1 = done(S.activation(winit, acol, ACT.Identity, scale=float(K), bias=-float(K * (N - 1))))
     t_s2 = done(S.activation(g0, pcol, ACT.Identity, scale=-76.0, bias=83.0))
     done(S.activation(nega, acol, ACT.Identity, scale=-BIG), t_s2)
     t_s3 = done(S.activation(top, tcol, ACT.Identity, bias=4.0 * TC))
-    wait("S", t_s2, t_c152)
+    wait("S", t_c80, t_s2)
     t_g1 = done(S.activation(g1, qcol, ACT.Identity, scale=4.0, bias=g0))
-    done(S.activation(T.csel[:], T.c152[:, 0:C], ACT.Relu, bias=nega), t_s3)
-    t_hp = fill(T.xb[:, 0:512], 512, 0.0)
-    for i in range(2):
-        fill(T.hb[:, 4 * LW * i:4 * (LW * i + PAD)], 4 * PAD, 0.0, t_hp)
+    done(S.activation(T.csel[:], T.c80[:], ACT.Relu, bias=nega), t_s3)
+    t_hp = fill(T.xb[:, 4 * C:512], 4 * PAD, 0.0)
     fill(T.zb[:, 0:4 * PAD], 4 * PAD, 0.0, t_hp)
-    t_d = fill(T.d0[:, 0:96:3], 32, HUGE)
-    fill(T.d1[:, 1:96:3], 32, HUGE, t_d)
+    t_d = fill(T.d0[:, 0:128:4], 32, HUGE)
+    fill(T.d1[:, 1:128:4], 32, HUGE, t_d)
+    fill(T.d1[:, 2:128:4], 32, HUGE, t_d)
     wait("S", t_jr)
-    done(S.activation(T.d1[:, 2:96:3], T.jr[:], ACT.Identity, bias=qcol), t_d)
-    t_xw = tok()
-    for b in RAW:
-        fill(T.dw[:, DW * b + 4 * C:DW * (b + 1)], TC, 0.0, t_xw)
-    wait("S", t_vals, *t_x)
-    for b in SUM:
-        done(S.activation(T.dw[:, DW * b + 4 * C:DW * (b + 1)], T.xs[:, b:4 * TC:4], ACT.Copy), t_xw)
-    t_tab = fill(T.tab[:, 4 * C:DW], TC, -1.0)
-    for s, d in enumerate(order):
-        done(S.activation(T.tab[:, C * s:C * s + C], T.vals[:, 0:C], ACT.Identity, scale=-0.25,
-                          bias=float(TC + C * d)), t_tab)
+    done(S.activation(T.d1[:, 3:128:4], T.jr[:], ACT.Identity, bias=qcol), t_d)
+    t_xw = fill(T.dw[:, DW * RAW + 4 * C:DW * (RAW + 1)], TC, 0.0)
+    wait("S", *t_x)
+    for b in range(4):
+        if b != RAW:
+            done(S.activation(T.dw[:, DW * b + 4 * C:DW * (b + 1)], T.xs[:, b:4 * TC:4], ACT.Copy), t_xw)
 
     tv = tok()
     for n, (j0, j1) in enumerate(runs):
@@ -218,42 +218,54 @@ def rank_program(g, core, T, topo):
     ev, od = T.pt[:, 0:TC:8], T.pt[:, 4:TC:8]
     t1 = done(V.tensor_tensor(T.mm[:], ev, od, OP.max))
     done(V.tensor_tensor(T.ww[:], ev, od, OP.is_ge), tv)
+    done(V.tensor_tensor(T.wn[:], ev, od, OP.is_lt), tv)
     wait("V", t1)
     done(V.tensor_tensor(T.ff[:, 0:36:2], T.mm[:, 0:36:2], T.mm[:, 1:36:2], OP.is_ge), tv)
     done(V.tensor_tensor(T.ff[:, 1:36:2], T.mm[:, 0:36:2], T.mm[:, 1:36:2], OP.is_lt), tv)
-    wait("V", tv, t_z)
-    done(V.tensor_tensor(T.fl[:, 0:TC:8], T.ff[:], T.ww[:], OP.mult), tv)
-    done(V.tensor_tensor(T.fl[:, 4:TC:8], T.ff[:], T.ww[:], OP.is_gt), tv)
-    wait("V", tv)
-    done(V.transpose(T.fr[:], T.fl[:]), tv)
+    wait("V", t_z, tv)
+    done(V.tensor_tensor(T.nf[:, 320:608:8], T.ff[:], T.wn[:], OP.is_le), tv)
+    done(V.tensor_tensor(T.nf[:, 324:608:8], T.ff[:], T.ww[:], OP.is_le), tv)
+    wait("V", t_pad, tv)
+    done(V.transpose(T.fr[:, 16:304], fl), tv)
     wait("V", t_g1, t_s1)
     t_gl = done(V.tensor_scalar(T.gl[:], T.ul[:, 0:5:4], g1, 151.0, OP.add, OP.min))
     wait("V", tv)
-    done(V.tensor_tensor_scan(T.cum[:], T.fr[:], T.fr[:], winit, OP.add, OP.max), tv)
-    wait("V", tv, t_pad)
-    done(V.tensor_tensor_scan(T.rr[:, 16:304], T.cum[:], T.fr[:], 0.0, OP.max, OP.mult), tv)
-    wait("V", tv)
-    done(V.transpose(T.tt[:, 0:320], T.rr[:, 0:320]), tv)
+    done(V.tensor_tensor_scan(T.rr[:, 16:304], T.fr[:, 16:304], T.ones[:, 0:TC], winit, OP.add, OP.subtract), tv)
+    t_sh = done(V.transpose(T.nf[:, 0:320], T.fr[:]))
+    wait("V", t_gl, tv)
+    t_ta = done(V.transpose(T.tt[:, 0:320], T.rr[:, 0:320]))
     done(V.transpose(T.tt[:, 320:608], T.rr[:, 16:304]), tv)
-    wait("V", tv, t_c152)
-    t8 = done(V.tensor_tensor_scan(T.s152[:], T.c152[:], T.tt[:, 0:608:4], 0.0, OP.min, OP.max))
-    wait("V", t8, t_gl)
+    wait("V", t_sh, t_ta)
+    t8 = done(V.tensor_tensor_scan(T.s152[:, 0:80], T.nf[:, 0:320:4], T.tt[:, 0:320:4], 0.0, OP.mult, OP.min))
+    wait("V", tv)
+    done(V.tensor_tensor_scan(T.s152[:, 80:152], T.nf[:, 320:608:4], T.tt[:, 320:608:4], 0.0, OP.mult, OP.min), t8)
+    wait("V", t8)
     places = T.s152[:].indirect(T.gl[:])
-    done(V.tensor_scalar(T.loff[:], places, 4.0, -4.0, OP.mult, OP.add), tv)
-    wait("V", tv, t_win, t_vals)
+    done(V.tensor_scalar(T.loff[:], places, -1.0, -1.0, OP.mult, OP.add), tv)
+    wait("V", t_win, t_vals, tv)
     done(V.tensor_copy(T.win[:].indirect(T.loff[:, 0:NL]), T.vals[:]), tv)
 
-    wait("S", t8, t_gl)
-    t_rb = done(S.activation(T.rb[:], places, ACT.Identity, bias=127.625))
-    done(S.activation(T.d1[:, 0:96:3], places, ACT.Identity, scale=4.0 * C), t_d)
-    done(S.activation(T.d0[:, 2:96:3], places, ACT.Relu, scale=16.0 * BIG, bias=-(16.0 * C + 14.0) * BIG), t_d)
+    slots = [order.index(N - 1 - e) for e in range(N)]
+    turn = 1 if (slots[0] + 1) % N == slots[1] else -1
+    wrap = ([e for e in range(N) if slots[e] != slots[0] + turn * e] + [N])[0]
+    assert slots == [slots[0] + turn * (e - N * (e >= wrap)) for e in range(N)]
+    over, per_e = 2 * BIG, float(turn * C - K) - 2 * BIG
+    wait("S", t_gl, t8)
+    t_rb = tok()
+    for k, (step, below) in enumerate(((K, 0.8 * K), (K, C + 0.5), (N * K, K * wrap - 100.0))):
+        done(S.activation(T.rb[:, 32 * k:32 * k + 32], places, ACT.Identity, scale=-1.0 / step,
+                          bias=WHOLE + 0.5 - below / step), t_rb)
+    done(S.activation(T.d1[:, 0:128:4], places, ACT.Identity, scale=-1.0), t_d)
     wait("S", t_rb)
-    done(S.activation(T.d0[:, 1:96:3], T.rb[:], ACT.Identity, scale=1.0 - 4 * C, bias=128.0 * (4 * C - 1) - 1), t_d)
+    for k, (col, by, plus) in enumerate(((1, per_e, C * slots[0] - 1.0), (3, over, 0.0), (2, -turn * N * C, 0.0))):
+        done(S.activation(T.d0[:, col:128:4], T.rb[:, 32 * k:32 * k + 32], ACT.Identity, scale=float(by),
+                          bias=plus - WHOLE * by), t_d)
 
-    wait("V", tv, t_s3)
+    wait("V", t_s3, t_hp, tv)
 
     def select(i, t=None):
-        return done(V.tensor_tensor_scan(T.sel[:, C * i:C * i + C], T.csel[:], T.win[:, i:4 * C:4], 0.0,
+        w0 = K * (N - 1 - order[i])
+        return done(V.tensor_tensor_scan(T.sel[:, C * i:C * i + C], T.csel[:], T.win[:, w0:w0 + C], 0.0,
                                          OP.min, OP.max), t)
 
     def offsets(lo, hi):
@@ -276,111 +288,113 @@ def rank_program(g, core, T, topo):
     wait("V", t_sa)
     t_oa = offsets(1, 2)
     select(3, t_sb)
+    t_sc = select(0)
     wait("V", t_oa)
-    t_ba = bundle("V", 20, 20 + CFG["g0"])
+    t_ba = bundle("V", 20, 34)
     wait("S", t_oa)
-    bundle("S", 20 + CFG["g0"], 40, t_ba)
+    bundle("S", 34, 40, t_ba)
     wait("V", t_sb)
     t_ob = offsets(2, 4)
-    wait("V", t_ba, t_hp)
-    t_q1 = pack(T.oq, T.op, 0, T.xb, F1 - PAD, 128)
-    wait("V", t_ob)
-    t_bb = bundle("V", 40, 40 + CFG["g12"])
-    wait("S", t_ob)
-    bundle("S", 40 + CFG["g12"], 80, t_bb)
-    t_sc = select(0)
     wait("V", t_sc)
     t_oc = offsets(0, 1)
+    wait("V", t_ba)
+    t_q1 = pack(T.oq, T.op, 0, T.xb, F1 - PAD, 128)
+    wait("S", t_ob)
+    t_bb = bundle("S", 54, 80)
+    wait("V", t_ob)
+    bundle("V", 40, 54, t_bb)
+    wait("V", t_q1, t_oc)
+    t_bc = bundle("V", 0, 12)
+    wait("S", t_q1, t_oc)
+    bundle("S", 12, 20, t_bc)
     wait("V", t_bb)
     t_q2 = pack(T.oq, T.op, 128, T.xb, F2, HW)
-    wait("S", t_oc, t_q1)
-    t_bc = bundle("S", CFG["g3"], 20)
-    wait("V", t_oc, t_q1)
-    bundle("V", 0, CFG["g3"], t_bc)
     wait("V", t_bc)
-    t_q3 = pack(T.lq, T.lp, 0, T.xb, 0, 128)
+    t_q3 = pack(T.lq, T.lp, C, T.xb, OWN, 128)
 
-    out_eng = near_eng[::len(near_eng) // CFG["near"]]
-    home_eng = near_eng[::len(near_eng) // CFG["nearh"]]
     wait("G", t_q1)
-    n_out1 = wave([(far1, far_eng, PAD, F1)], T.oq, T.op, T.lq, T.lp, T.sem.out1)
+    out1 = wave([(far1, far_eng, PAD, 0)], T.oq, T.op, T.lq, T.lp, T.sem.out1)
     wait("G", t_q2)
-    n_out2 = wave([(far2, far_eng, 128, F2), (near, out_eng, 128 + C, NR)], T.oq, T.op, T.lq, T.lp, T.sem.out2)
+    out2 = wave([(far2, far_eng, 128, F2), (near, near_eng, 128 + C, NR)], T.oq, T.op, T.lq, T.lp, T.sem.out2)
     g.sem_inc(t_go["sem"], 1)
     t_go["n"] += 1
+    t_tab = done(g.iota(T.tab[:, 4 * C:DW], [[0, TC]], -1, 0, **fl_ok))
+    for s, d in enumerate(order):
+        done(g.iota(T.tab[:, C * s:C * s + C], [[1, C]], C * d, 0, **fl_ok), t_tab)
 
-    one, two = (lambda c: (c - PAD, 128, PAD)), (lambda c: (c, HW, 0))
-    passes = {"o": one(OWN), "F": one(F1), "W": two(F2), "1": one(F1), "2": two(F2)}
+    width = {"o": C, "F": C, "W": HW, "1": C, "2": HW}
+    x_col = {"o": C, "F": 0, "W": F2}
+    h_col = {"o": C, "F": 0, "W": 2 * HW, "1": 0, "2": 2 * HW}
+    z_col = {"1": PAD, "2": PAD + C, "o": PAD + 3 * C}
     banks = {"oA0": 4, "oA1": 0, "FA0": 4, "FA1": 0, "WA0": 4, "WA1": 0, "1C": 4, "2C": 0, "oC": 4}
-    before = {"oA1": None, "oA0": None, "FA0": "o0", "FA1": "o1", "WA0": "F0", "WA1": "F1", "1C": "W0", "2C": "W1",
+    before = {"oA0": None, "oA1": None, "FA0": "o0", "FA1": "o1", "WA0": "F0", "WA1": "F1", "1C": "W0", "2C": "W1",
               "oC": "12"}
-    made_in = {"o": "o", "1": "F", "2": "W"}
+    uses = {"oA0": 1, "oA1": 1, "FA0": 2, "FA1": 2, "WA0": 3, "WA1": 3, "1C": 4, "2C": 4, "oC": 5}
+    arrives = {"FA0": out1, "WA0": out2}
     stage_of = {p + str(n): p + ("A%d" % n if n < 2 else "C") for p in "oFW12" for n in range(3)}
     t_bank = [tok() for b in range(8)]
-    uses = {}
-    count = [0] * 8
-    for st in ["oA0", "oA1"] + CFG["pe"].split() + ["oC"]:
-        st = st[:2] if st[1] == "C" else st
-        if st not in uses:
-            for b in range(4):
-                count[banks[st] + b] += 1
-            uses[st] = count[banks[st]]
-    t_ev = {k: tok() for k in ("o0", "o1", "o2", "F0", "F1", "W0", "W1", "12", "22")}
-    t_q = {k: tok() for k in t_ev}
+    tiles = ("o0", "o1", "o2", "F0", "F1", "W0", "W1", "12", "22")
+    t_ev = {k: (tok(), tok()) for k in tiles}
+    t_q = {k: tok() for k in tiles[2:]}
 
-    def z_col(c):
-        return c - C if c >= F1 else c + 3 * C
+    def emptied(q, k, halves=(0, 1)):
+        for h in halves:
+            wait_for(q, t_ev[k][h], 2)
 
-    def product(q, s, i, b, st, mq, ms, c0, start, stop):
-        k = 512 * i + 128 * b
-        m0, n, _f = passes[st[0]]
-        ins = PE.matmul_mx(bank(banks[st] + b, n), q[:, k:k + 128], s[:, k:k + 128], mq[:, c0 + m0:c0 + m0 + n],
-                           ms[:, c0 + m0:c0 + m0 + n], start, stop)
+    def product(q, s, i, b, st, mq, ms, m0, start, stop):
+        k, n = 512 * i + 128 * b, max(128, width[st[0]])
+        if before[st] is not None:
+            emptied("PE", before[st], (b // 2,))
+        ins = PE.matmul_mx(bank(banks[st] + b, n), q[:, k:k + 128], s[:, k:k + 128], mq[:, m0:m0 + n],
+                           ms[:, m0:m0 + n], start, stop)
         if stop:
             done(ins, t_bank[banks[st] + b])
 
     def layer(st):
-        key = st[:2] if st[1] == "C" else st
-        if before[key] is not None:
-            wait_for("PE", t_ev[before[key]], 4)
+        key, p = st[:2] if st[1] == "C" else st, st[0]
+        if st in arrives:
+            PE.wait_ge(*arrives[st])
         if st[1] == "A":
             for b in range(4):
-                product(T.aq, T.asc, int(st[2]), b, st, T.lq, T.lp, 0, True, True)
+                product(T.aq, T.asc, int(st[2]), b, st, T.lq, T.lp, x_col[p], True, True)
             return
         steps = [(int(st[2]), b) for b in range(4)] if len(st) == 3 else [(i, b) for b in range(4) for i in range(2)]
         for i, b in steps:
-            wait_for("PE", t_q[made_in[st[0]] + str(i)], 1)
-            wait("PE", t_c if 512 * i + 128 * b < early else t_c2)
-            product(T.cq, T.csc, i, b, key, T.hq, T.hp, LW * i, i == 0, i == 1)
+            if p != "o":
+                wait_for("PE", t_q[("W" if p == "2" else "F") + str(i)], 1)
+            wait("PE", t_c if 512 * i + 128 * b < EARLY else t_c2)
+            product(T.cq, T.csc, i, b, key, T.hq, T.hp, h_col[p] + HW * i, i == 0, i == 1)
 
     def evict(q, k, bs):
-        st, n = stage_of[k], int(k[1])
-        m0, w, f = passes[k[0]]
+        st, p, n = stage_of[k], k[0], int(k[1])
+        w = width[p]
         for b in bs:
             wait_for(q, t_bank[banks[st] + b], uses[st])
-            src = bank(banks[st] + b, w, f)
+            src = bank(banks[st] + b, w)
             if n < 2:
-                c = LW * n + m0 + f
-                dst = T.hb[:, 4 * c + b:4 * (c + w - f):4]
+                c = h_col[p] + HW * n
+                dst = T.hb[:, 4 * c + b:4 * (c + w):4]
                 ins = (V.tensor_scalar(dst, src, 0.0, 0.0625, OP.max, OP.mult) if q == "V" else
                        S.activation(dst, src, ACT.Relu, scale=0.0625))
             else:
-                c = z_col(m0 + f)
-                dst = T.zb[:, 4 * c + b:4 * (c + w - f):4]
+                dst = T.zb[:, 4 * z_col[p] + b:4 * (z_col[p] + w):4]
                 ins = (V.tensor_scalar(dst, src, 0.0625, None, OP.mult) if q == "V" else
                        S.activation(dst, src, ACT.Identity, scale=0.0625))
-            done(ins, t_ev[k])
+            done(ins, t_ev[k][b // 2])
 
     def quantise(k):
-        n = int(k[1])
-        m0, w, f = passes[k[0]]
-        wait_for("V", t_ev[k], 4)
+        p, n = k[0], int(k[1])
+        if p == "F":
+            emptied("V", "o%d" % n)
+        emptied("V", k)
         if n < 2:
-            pack(T.hq, T.hp, LW * n + m0, T.hb, LW * n + m0, w, t_q[k])
-        elif k[0] == "o":
-            pack(T.zl, T.zlp, 0, T.zb, LW - 128, 128, t_q[k])
+            pack(T.hq, T.hp, h_col[p] + HW * n, T.hb, h_col[p] + HW * n, HW, t_q[k])
+        elif p == "o":
+            pack(T.zl, T.zlp, 0, T.zb, z_col[p] - PAD, 128, t_q[k])
+        elif p == "1":
+            pack(T.zq, T.zp, 0, T.zb, 0, 128, t_q[k])
         else:
-            pack(T.zq, T.zp, HW * (int(k[0]) - 1), T.zb, z_col(m0 + f) - f, w, t_q[k])
+            pack(T.zq, T.zp, 128, T.zb, z_col[p], HW, t_q[k])
 
     t_qe = tok()
 
@@ -391,54 +405,40 @@ def rank_program(g, core, T, topo):
             elif w[0] == "q":
                 quantise(w[1:3])
             else:
-                b0, b1 = int(w[1]), int(w[2])
                 wait("V", t_e)
-                pack(T.eq, T.esc, 128 * b0, T.ebf, 128 * b0, 128 * (b1 - b0), t_qe)
+                for b in [int(b) for b in w[1:]]:
+                    e0 = EW * (b % 2) + 2 - b // 2 * 2
+                    done(V.quantize_mx(T.eq[:, 128 * b:128 * b + 128], T.esc[:, 128 * b:128 * b + 128],
+                                       T.ebf[:, e0:e0 + 512]), t_qe)
 
-    wait("PE", tv, t_a, t_q3)
-    layer("oA0")
-    layer("oA1")
     wait("V", t_d)
-    done(V.tensor_tensor_scan(T.d2[:], T.d0[:, 0:3 * NL], T.d1[:, 0:3 * NL], 0.0, OP.add, OP.min), tv)
-    evict("S", "o0", (0, 1, 2))
-    evict("V", "o0", (3,))
+    done(V.tensor_tensor_scan(T.d2[:], T.d0[:, 0:4 * NL], T.d1[:, 0:4 * NL], 0.0, OP.add, OP.min), tv)
+    first, rest = ON_VECTOR.split(" ", 1)
+    follow("V", first)
     wait("V", tv)
-    t_h = done(V.tensor_copy(T.hoff[:], T.d2[:, 2:3 * NL:3]))
-    quantise("o0")
-    evict("S", "o1", (0, 1, 2))
-    evict("V", "o1", (3,))
-    quantise("o1")
-    wait("V", t_q["o0"], t_q["o1"])
+    t_h = done(V.tensor_copy(T.hoff[:], T.d2[:, 3:4 * NL:4]))
 
-    for st in CFG["pe"].split():
-        if st == "FA0":
-            PE.wait_ge(T.sem.out1, n_out1)
-        if st == "WA0":
-            PE.wait_ge(T.sem.out2, n_out2)
+    wait("PE", t_a, t_q3)
+    for st in ON_TENSOR.split():
         layer(st)
-    follow("V", CFG["v"])
-    follow("S", CFG["s"])
+    follow("V", rest)
+    follow("S", ON_SCALAR)
 
     wait("G", t_q["12"])
-    n_home1 = wave([(far1, far_eng, PAD, F1)], T.zq, T.zp, T.zl, T.zlp, T.sem.home1)
+    home1 = wave([(far1, far_eng, PAD, F1)], T.zq, T.zp, T.zl, T.zlp, T.sem.home1)
     wait("G", t_q["22"])
-    n_home2 = wave([(far2, far_eng, HW, F2), (near, home_eng, HW + C, NR)], T.zq, T.zp, T.zl, T.zlp, T.sem.home2)
+    home2 = wave([(far2, far_eng, 128, F2), (near, near_eng, 128 + C, NR)], T.zq, T.zp, T.zl, T.zlp, T.sem.home2)
 
-    layer("oC")
-    follow("S", CFG["so"])
-    follow("V", CFG["vo"])
-    wait("S", t_h, t_tab)
+    wait("S", t_h, t_tab, t_xw)
     t_olr = done(S.activation(T.olr[:], T.tab[:].indirect(T.hoff[:]), ACT.Copy))
-    wait("SY", t_olr)
-    t_out = done(SY.dma_start(T.ol[:], T.olr[0:128:16, :]), k=16)
 
     def decode(b0, s, ts):
         m0 = PAD + C * s
-        for b in CFG["dec"]:
+        for b in UNPACK:
             t = done(PE.matmul_mx(bank(b0 + b, HW), T.eq[:, 128 * b:128 * b + 128], T.esc[:, 128 * b:128 * b + 128],
                                   T.zl[:, m0:m0 + HW], T.zlp[:, m0:m0 + HW], True, True), t_bank[b0 + b])
             dst, src = T.dw[:, DW * b + C * s:DW * b + C * s + HW], bank(b0 + b, HW)
-            if b in RAW:
+            if b == RAW:
                 wait("S", t)
                 done(S.activation(dst, src, ACT.Copy), ts[b])
             else:
@@ -446,17 +446,21 @@ def rank_program(g, core, T, topo):
                 done(V.tensor_tensor(dst, src, T.xb[:, 4 * m0 + b:4 * (m0 + HW):4], OP.add), ts[b])
 
     t_first = tok()
-    wait("V", t_v)
-    t_qv = done(V.quantize_mx(T.vq[:], T.vsc[:], T.vs[:]))
     t_dn = [tok() for b in range(4)]
-    wait("PE", t_qe, t_q["o2"], t_ev["22"])
-    PE.wait_ge(T.sem.home1, n_home1)
+    wait("V", t_h, t_xw, t_v)
+    t_qv = done(V.quantize_mx(T.vq[:], T.vsc[:], T.vs[:]))
+    wait("PE", t_qe)
+    emptied("PE", "22")
+    PE.wait_ge(*home1)
+    wait("PE", t_q["o2"])
     decode(0, 0, [t_first] * 4)
-    wait("PE", t_ev["o2"])
-    PE.wait_ge(T.sem.home2, n_home2)
+    wait("SY", t_olr, t_first)
+    t_out = done(SY.dma_start(T.ol[:], T.olr[0:128:16, :]), k=16)
+    emptied("PE", "o2")
+    PE.wait_ge(*home2)
     decode(4, 2, t_dn)
-    wait("V", t_h, t_first, t_xw)
-    wait("S", t_h, t_first, t_xw)
+    wait("V", t_first)
+    wait("S", t_first)
     wait("PE", t_first, t_qv)
 
     ty = [tok(), tok()]
@@ -465,36 +469,19 @@ def rank_program(g, core, T, topo):
         dst = T.yb[:, 64 * c0 + b:64 * c1:4]
         src = T.dw[:, DW * b:DW * (b + 1)].indirect(T.hoff[:, c0:c1])
         wait(q, t_dn[b])
-        if b in RAW:
+        if b == RAW:
             done(V.tensor_tensor(dst, src, T.xs[:, 64 * c0 + b:64 * c1:4], OP.add), ty[n])
         else:
             gather(q, dst, src, ty[n])
 
-    def shares(n):
-        c0, c1 = runs[n][0] // 16, runs[n][1] // 16
-        out = [("V", b, c0, c1) for b in RAW]
-        for b in [b for b in CFG["dec"] if b in SUM]:
-            mine = [(a, z) for bb, a, z in CFG["yv"] if bb == b and c0 <= a < c1]
-            if not mine:
-                out.append(("S", b, c0, c1))
-                continue
-            a, z = mine[0]
-            out.append(("V", b, a, z))
-            if a > c0:
-                out.append(("S", b, c0, a))
-            if z < c1:
-                out.append(("S", b, z, c1))
-        return out
-
-    for n in range(2):
-        for q, b, c0, c1 in shares(n):
-            if q == "S":
-                pick_y(q, n, b, c0, c1)
+    mid = HW // 16
+    for share in ((0, 1, 0, mid), (0, 2, 0, mid), (1, 1, mid, NL), (1, 2, mid, NL), (1, 3, mid + 2, NL)):
+        pick_y("S", *share)
+    on_vector = (((0, RAW, 0, mid), (0, 3, 0, mid), (1, RAW, mid, NL)), ((1, 3, mid, mid + 2),))
     tq, tm = [None, None], [None, None]
     for n, (j0, j1) in enumerate(runs):
-        for q, b, c0, c1 in shares(n):
-            if q == "V":
-                pick_y(q, n, b, c0, c1)
+        for share in on_vector[n]:
+            pick_y("V", *share)
         wait("V", ty[n])
         tq[n] = pack(T.yq, T.ysc, j0, T.yb, j0, j1 - j0)
         wait("PE", tq[n])

from concourse.bass import DstId, RemoteDMATransfer
from concourse.mybir import dt, AluOpType, ActivationFunctionType

N, TC, C = 4, 288, 80
HW = 2 * C
PAD = 128 - C
LW = PAD + 4 * C
DW = 4 * C + TC
K = 512
BIG = 2048.0
HUGE = 512 * BIG
WHOLE = 192.0
NL = TC // 16
EW = 528
EARLY = 640
Q4, U8, BF, F32, I32, U16 = "float8_e4m3fn_x4", "uint8", "bfloat16", "float32", "int32", "uint16"
F16 = "float16"
RAW = 0
UNPACK = (1, 0, 2, 3)

ON_TENSOR = "oA0 oA1 FA0 FA1 WA0 WA1 1C 2C0 2C1 oC"
ON_VECTOR = ("eo0:13 eo1:13 eF0:13 qF0 eF1:3 eW0:1 qF1 eW0:3 qW0 eW1:3 qW1 e12:3 q12 E0 e22:13 q22 E123 "
             "eo2:3 qo2")
ON_SCALAR = "eo0:02 eo1:02 eF0:02 eF1:012 eW0:02 eW1:012 e12:012 e22:02 eo2:012"


def _sb(n, d):
    return ("sbuf", [128, n], d)


SCRATCH = {
    "xs": _sb(4 * TC, BF), "us": _sb(512, BF), "vs": _sb(512, BF),
    "aq": _sb(1024, Q4), "asc": _sb(1024, U8), "cq": _sb(1024, Q4), "csc": _sb(1024, U8),
    "xq": _sb(TC, Q4), "xsc": _sb(TC, U8),
    "uq": _sb(128, Q4), "usc": _sb(128, U8), "uq2": _sb(128, Q4), "usc2": _sb(128, U8),
    "vq": _sb(128, Q4), "vsc": _sb(128, U8),
    "ones": _sb(514, BF), "ebf": _sb(2 * EW, BF), "eq": _sb(512, Q4), "esc": _sb(512, U8),
    "ip": _sb(2, I32), "ci": _sb(4, I32), "cf": _sb(4, F32), "cs": _sb(5, F32), "ul": _sb(8, I32),
    "uoff": _sb(8, U16), "gl": _sb(2, U16),
    "csel": _sb(C, F32), "c80": _sb(C, F32), "vals": _sb(TC, F32),
    "pt": _sb(TC, F32), "mm": _sb(36, F32), "ww": _sb(36, F32), "wn": _sb(36, F32), "ff": _sb(36, F32),
    "nf": _sb(608, BF), "fr": _sb(320, BF), "rr": _sb(320, F16), "tt": _sb(608, F16),
    "s152": _sb(152, F32), "loff": _sb(32, U16), "win": _sb(N * K, F32), "sel": _sb(4 * C, F32),
    "goff": _sb(C, U16), "xb": _sb(4 * LW, BF),
    "oq": _sb(128 + HW, Q4), "op": _sb(128 + HW, U8), "lq": _sb(LW, Q4), "lp": _sb(LW, U8),
    "hb": _sb(16 * HW, BF), "hq": _sb(4 * HW, Q4), "hp": _sb(4 * HW, U8),
    "zb": _sb(4 * LW, BF), "zq": _sb(128 + HW, Q4), "zp": _sb(128 + HW, U8), "zl": _sb(LW, Q4), "zlp": _sb(LW, U8),
    "jr": _sb(32, F32), "d0": _sb(128, F32), "d1": _sb(128, F32), "d2": _sb(4 * NL, F32), "rb": _sb(96, BF),
    "hoff": _sb(NL, U16), "tab": _sb(DW, F32), "olr": _sb(TC, F32),
    "dw": _sb(4 * DW, BF), "yb": _sb(4 * TC, BF), "yq": _sb(TC, Q4), "ysc": _sb(TC, U8), "yo": _sb(TC, F32),
    "pp": ("psum", [128, 4096], F32),
}
SEMAPHORES = ["out1", "out2", "home1", "home2", "sent"] + ["s%d" % i for i in range(145)]

OP = AluOpType
ACT = ActivationFunctionType


def rank_program(g, core, T, topo):
    r = T.rank_of(core)
    if r is None:
        return
    cores = list(T.cores)
    V, S, PE, SY = g.vector, g.scalar, g.tensor, g.sync
    queues = {"V": V, "S": S, "PE": PE, "SY": SY, "G": g}
    toks = []

    def tok():
        t = {"sem": T.sem["s%d" % len(toks)], "n": 0, "w": {}}
        toks.append(t)
        return t

    def done(ins, t=None, k=1):
        if t is None:
            t = tok()
        ins.then_inc(t["sem"], k)
        t["n"] += k
        return t

    def wait_for(q, t, n):
        if t["w"].get(q, 0) < n:
            queues[q].wait_ge(t["sem"], n)
            t["w"][q] = n

    def wait(q, *ts):
        for t in ts:
            wait_for(q, t, t["n"])

    near = [d for d in range(N) if d != r and topo.chip(cores[d]) == topo.chip(core)][0]
    others = [d for d in range(N) if topo.chip(cores[d]) != topo.chip(core)]
    far1 = [d for d in others if topo.die(cores[d]) != topo.die(core)][0]
    far2 = [d for d in others if d != far1][0]
    order = [r, far1, far2, near]
    far_eng = topo.engines(core, cores[far1])
    near_eng = [e for e in topo.engines(core, cores[near]) if e not in far_eng][::2]
    sent = [0]

    def b8(ap):
        return ap.bitcast(dt.uint8)

    def send(trs, sem):
        out = []
        for d, es, src, dst in trs:
            rid, pid, _se = topo.addr(cores[d])
            m = 0
            for e in es:
                m |= 1 << e
            out.append(RemoteDMATransfer(dst_ids=[DstId(rid=rid, pnc=pid)], dma_engine_mask=m, remote_sem=sem,
                                         src=src, dst=dst))
            sent[0] += len(es)
        g.remote_dma_fused(out, local_sem=T.sem.sent)

    def wave(items, sq, sp, dq, dp, sem):
        send([(d, es, b8(sq[:, a:a + C]), b8(dq[:, z:z + C])) for d, es, a, z in items], sem)
        send([(d, es, sp[:, a:a + C], dp[:, z:z + C]) for d, es, a, z in items], sem)
        return sem, 2 * sum(len(es) for d, es, a, z in items)

    def bank(b, n, c0=0):
        return T.pp[:, 512 * b + c0:512 * b + n]

    def fill(dst, n, value, t=None):
        return done(S.activation(dst, T.ones[:, 0:n], ACT.Identity, scale=value), t)

    OWN, F1, F2, NR = [PAD + C * s for s in range(N)]

    runs = ((0, HW), (HW, TC))
    t_u = done(SY.dma_start(T.us[:], T.u[:]), k=16)
    t_x = [done(SY.dma_start(T.xs[:, 4 * j0:4 * j1], T.x[:, 4 * j0:4 * j1]), k=16) for j0, j1 in runs]
    t_a = done(SY.dma_start(b8(T.aq[:]), T.ac[:]), k=16)
    done(SY.dma_start(T.asc[:], T.ap[:]), t_a, 16)
    t_c = done(SY.dma_start(T.csc[:], T.cp[:]), k=16)
    done(SY.dma_start(b8(T.cq[:, 0:EARLY]), T.cc[:, 0:4 * EARLY]), t_c, 16)
    t_go = tok()
    wait_for("SY", t_go, 1)
    t_c2 = done(SY.dma_start(b8(T.cq[:, EARLY:1024]), T.cc[:, 4 * EARLY:4096]), k=16)
    t_v = done(SY.dma_start(T.vs[:], T.v[:]), k=16)

    fl_ok = {"allow_small_or_imprecise_dtypes": True}
    t_ip = done(g.iota(T.ip[:, 0:1], [[0, 1]], 0, 1))
    t_ul = done(g.iota(T.ul[:], [[16, 8]], 0, 0))
    t_ip2 = done(g.iota(T.ip[:, 1:2], [[0, 1]], 0, 17))
    t_c80 = done(g.iota(T.c80[:], [[0, C // 4], [int(BIG), 4]], 0, 0, **fl_ok))
    t_vals = done(g.iota(T.vals[:], [[-4, TC]], 4 * TC, 0, **fl_ok))
    t_jr = done(g.iota(T.jr[:], [[16, 32]], 4 * C, 0, **fl_ok))

    acol, tcol, qcol, pcol = [T.cf[:, k:k + 1] for k in range(4)]
    winit, nega, top, g0, g1 = [T.cs[:, k:k + 1] for k in range(5)]
    t_ones = done(V.memset(T.ones[:], 1.0))
    wait("V", t_ip)
    t_l0 = done(V.tensor_scalar(T.ci[:, 0:1], T.ip[:, 0:1], 2, 3, OP.logical_shift_right, OP.bitwise_and))
    t_l1 = done(V.tensor_scalar(T.ci[:, 1:2], T.ip[:, 0:1], 3, None, OP.bitwise_and))
    done(V.tensor_scalar(T.ci[:, 2:3], T.ip[:, 0:1], 15, None, OP.bitwise_and), t_l1)
    wait("V", t_l0)
    t_l2 = done(V.tensor_copy(T.cf[:, 0:1], T.ci[:, 0:1]))
    wait("V", t_ip2)
    done(V.tensor_scalar(T.ci[:, 3:4], T.ip[:, 1:2], 4, 1, OP.logical_shift_right, OP.bitwise_and), t_l1)
    wait("V", t_ones)
    t_pad = done(V.tensor_copy(T.rr[:], T.ones[:, 0:320]))
    wait("V", t_ul, t_l2)
    t_uo = done(V.tensor_scalar(T.uoff[:], T.ul[:], acol, None, OP.add))
    wait("V", t_l1)
    done(V.tensor_copy(T.cf[:, 1:4], T.ci[:, 1:4]), t_l2)
    done(V.tensor_copy(T.fr[:], T.ones[:, 0:320]), t_pad)

    fl = T.nf[:, 320:608]
    wait("S", t_ones)
    t_z = fill(fl, TC, 0.0)
    t_win = tok()
    for e in range(N):
        fill(T.win[:, K * e:K * e + C], C, 4.0, t_win)

    wait("G", t_ones)
    t_e = tok()
    for k in range(2):
        done(g.affine_select(T.ebf[:, EW * k:EW * k + 514], T.ones[:], [[1, 514]], OP.is_equal, 0.0, -2 - k, -4), t_e)

    wait("V", t_u)
    t_qu = done(V.quantize_mx(T.uq[:], T.usc[:], T.us[:]))
    wait("V", t_uo, t_qu)
    t_pu = done(V.tensor_copy(T.uq2[:].bitcast(dt.uint32), T.uq[:].bitcast(dt.uint32).indirect(T.uoff[:])))
    wait("S", t_uo, t_qu)
    done(S.activation(T.usc2[:], T.usc[:].indirect(T.uoff[:]), ACT.Copy), t_pu)
    wait("PE", t_pu)
    t_p = []
    for n, (j0, j1) in enumerate(runs):
        wait("V", t_x[n])
        t_qx = done(V.quantize_mx(T.xq[:, j0:j1], T.xsc[:, j0:j1], T.xs[:, 4 * j0:4 * j1]))
        wait("PE", t_qx)
        t_p.append(done(PE.matmul_mx(bank(n, j1 - j0), T.uq2[:], T.usc2[:], T.xq[:, j0:j1], T.xsc[:, j0:j1],
                                     True, True)))

    wait("S", t_l2)
    t_s1 = done(S.activation(winit, acol, ACT.Identity, scale=float(K), bias=-float(K * (N - 1))))
    t_s2 = done(S.activation(g0, pcol, ACT.Identity, scale=-76.0, bias=83.0))
    done(S.activation(nega, acol, ACT.Identity, scale=-BIG), t_s2)
    t_s3 = done(S.activation(top, tcol, ACT.Identity, bias=4.0 * TC))
    wait("S", t_c80, t_s2)
    t_g1 = done(S.activation(g1, qcol, ACT.Identity, scale=4.0, bias=g0))
    done(S.activation(T.csel[:], T.c80[:], ACT.Relu, bias=nega), t_s3)
    t_hp = fill(T.xb[:, 4 * C:512], 4 * PAD, 0.0)
    fill(T.zb[:, 0:4 * PAD], 4 * PAD, 0.0, t_hp)
    t_d = fill(T.d0[:, 0:128:4], 32, HUGE)
    fill(T.d1[:, 1:128:4], 32, HUGE, t_d)
    fill(T.d1[:, 2:128:4], 32, HUGE, t_d)
    wait("S", t_jr)
    done(S.activation(T.d1[:, 3:128:4], T.jr[:], ACT.Identity, bias=qcol), t_d)
    t_xw = fill(T.dw[:, DW * RAW + 4 * C:DW * (RAW + 1)], TC, 0.0)
    wait("S", *t_x)
    for b in range(4):
        if b != RAW:
            done(S.activation(T.dw[:, DW * b + 4 * C:DW * (b + 1)], T.xs[:, b:4 * TC:4], ACT.Copy), t_xw)

    tv = tok()
    for n, (j0, j1) in enumerate(runs):
        wait("V", t_p[n])
        done(V.transpose(T.pt[:, j0:j1], bank(n, j1 - j0)), tv)
    wait("V", tv)
    ev, od = T.pt[:, 0:TC:8], T.pt[:, 4:TC:8]
    t1 = done(V.tensor_tensor(T.mm[:], ev, od, OP.max))
    done(V.tensor_tensor(T.ww[:], ev, od, OP.is_ge), tv)
    done(V.tensor_tensor(T.wn[:], ev, od, OP.is_lt), tv)
    wait("V", t1)
    done(V.tensor_tensor(T.ff[:, 0:36:2], T.mm[:, 0:36:2], T.mm[:, 1:36:2], OP.is_ge), tv)
    done(V.tensor_tensor(T.ff[:, 1:36:2], T.mm[:, 0:36:2], T.mm[:, 1:36:2], OP.is_lt), tv)
    wait("V", t_z, tv)
    done(V.tensor_tensor(T.nf[:, 320:608:8], T.ff[:], T.wn[:], OP.is_le), tv)
    done(V.tensor_tensor(T.nf[:, 324:608:8], T.ff[:], T.ww[:], OP.is_le), tv)
    wait("V", t_pad, tv)
    done(V.transpose(T.fr[:, 16:304], fl), tv)
    wait("V", t_g1, t_s1)
    t_gl = done(V.tensor_scalar(T.gl[:], T.ul[:, 0:5:4], g1, 151.0, OP.add, OP.min))
    wait("V", tv)
    done(V.tensor_tensor_scan(T.rr[:, 16:304], T.fr[:, 16:304], T.ones[:, 0:TC], winit, OP.add, OP.subtract), tv)
    t_sh = done(V.transpose(T.nf[:, 0:320], T.fr[:]))
    wait("V", t_gl, tv)
    t_ta = done(V.transpose(T.tt[:, 0:320], T.rr[:, 0:320]))
    done(V.transpose(T.tt[:, 320:608], T.rr[:, 16:304]), tv)
    wait("V", t_sh, t_ta)
    t8 = done(V.tensor_tensor_scan(T.s152[:, 0:80], T.nf[:, 0:320:4], T.tt[:, 0:320:4], 0.0, OP.mult, OP.min))
    wait("V", tv)
    done(V.tensor_tensor_scan(T.s152[:, 80:152], T.nf[:, 320:608:4], T.tt[:, 320:608:4], 0.0, OP.mult, OP.min), t8)
    wait("V", t8)
    places = T.s152[:].indirect(T.gl[:])
    done(V.tensor_scalar(T.loff[:], places, -1.0, -1.0, OP.mult, OP.add), tv)
    wait("V", t_win, t_vals, tv)
    done(V.tensor_copy(T.win[:].indirect(T.loff[:, 0:NL]), T.vals[:]), tv)

    slots = [order.index(N - 1 - e) for e in range(N)]
    turn = 1 if (slots[0] + 1) % N == slots[1] else -1
    wrap = ([e for e in range(N) if slots[e] != slots[0] + turn * e] + [N])[0]
    assert slots == [slots[0] + turn * (e - N * (e >= wrap)) for e in range(N)]
    over, per_e = 2 * BIG, float(turn * C - K) - 2 * BIG
    wait("S", t_gl, t8)
    t_rb = tok()
    for k, (step, below) in enumerate(((K, 0.8 * K), (K, C + 0.5), (N * K, K * wrap - 100.0))):
        done(S.activation(T.rb[:, 32 * k:32 * k + 32], places, ACT.Identity, scale=-1.0 / step,
                          bias=WHOLE + 0.5 - below / step), t_rb)
    done(S.activation(T.d1[:, 0:128:4], places, ACT.Identity, scale=-1.0), t_d)
    wait("S", t_rb)
    for k, (col, by, plus) in enumerate(((1, per_e, C * slots[0] - 1.0), (3, over, 0.0), (2, -turn * N * C, 0.0))):
        done(S.activation(T.d0[:, col:128:4], T.rb[:, 32 * k:32 * k + 32], ACT.Identity, scale=float(by),
                          bias=plus - WHOLE * by), t_d)

    wait("V", t_s3, t_hp, tv)

    def select(i, t=None):
        w0 = K * (N - 1 - order[i])
        return done(V.tensor_tensor_scan(T.sel[:, C * i:C * i + C], T.csel[:], T.win[:, w0:w0 + C], 0.0,
                                         OP.min, OP.max), t)

    def offsets(lo, hi):
        return done(V.tensor_scalar(T.goff[:, 20 * lo:20 * hi], T.sel[:, C * lo + 3:C * hi:4], -1.0, top,
                                    OP.mult, OP.add))

    def gather(q, dst, src, t=None):
        if q == "V":
            return done(V.tensor_copy(dst, src), t)
        return done(S.activation(dst, src, ACT.Copy), t)

    def bundle(q, c0, c1, t=None):
        return gather(q, T.xb[:, 4 * PAD + 16 * c0:4 * PAD + 16 * c1], T.xs[:].indirect(T.goff[:, c0:c1]), t)

    def pack(q, s, c0, src, s0, n, t=None):
        return done(V.quantize_mx(q[:, c0:c0 + n], s[:, c0:c0 + n], src[:, 4 * s0:4 * (s0 + n)]), t)

    t_sa = select(1)
    t_sb = select(2)
    wait("V", t_sa)
    t_oa = offsets(1, 2)
    select(3, t_sb)
    t_sc = select(0)
    wait("V", t_oa)
    t_ba = bundle("V", 20, 34)
    wait("S", t_oa)
    bundle("S", 34, 40, t_ba)
    wait("V", t_sb)
    t_ob = offsets(2, 4)
    wait("V", t_sc)
    t_oc = offsets(0, 1)
    wait("V", t_ba)
    t_q1 = pack(T.oq, T.op, 0, T.xb, F1 - PAD, 128)
    wait("S", t_ob)
    t_bb = bundle("S", 54, 80)
    wait("V", t_ob)
    bundle("V", 40, 54, t_bb)
    wait("V", t_q1, t_oc)
    t_bc = bundle("V", 0, 12)
    wait("S", t_q1, t_oc)
    bundle("S", 12, 20, t_bc)
    wait("V", t_bb)
    t_q2 = pack(T.oq, T.op, 128, T.xb, F2, HW)
    wait("V", t_bc)
    t_q3 = pack(T.lq, T.lp, C, T.xb, OWN, 128)

    wait("G", t_q1)
    out1 = wave([(far1, far_eng, PAD, 0)], T.oq, T.op, T.lq, T.lp, T.sem.out1)
    wait("G", t_q2)
    out2 = wave([(far2, far_eng, 128, F2), (near, near_eng, 128 + C, NR)], T.oq, T.op, T.lq, T.lp, T.sem.out2)
    g.sem_inc(t_go["sem"], 1)
    t_go["n"] += 1
    t_tab = done(g.iota(T.tab[:, 4 * C:DW], [[0, TC]], -1, 0, **fl_ok))
    for s, d in enumerate(order):
        done(g.iota(T.tab[:, C * s:C * s + C], [[1, C]], C * d, 0, **fl_ok), t_tab)

    width = {"o": C, "F": C, "W": HW, "1": C, "2": HW}
    x_col = {"o": C, "F": 0, "W": F2}
    h_col = {"o": C, "F": 0, "W": 2 * HW, "1": 0, "2": 2 * HW}
    z_col = {"1": PAD, "2": PAD + C, "o": PAD + 3 * C}
    banks = {"oA0": 4, "oA1": 0, "FA0": 4, "FA1": 0, "WA0": 4, "WA1": 0, "1C": 4, "2C": 0, "oC": 4}
    before = {"oA0": None, "oA1": None, "FA0": "o0", "FA1": "o1", "WA0": "F0", "WA1": "F1", "1C": "W0", "2C": "W1",
              "oC": "12"}
    uses = {"oA0": 1, "oA1": 1, "FA0": 2, "FA1": 2, "WA0": 3, "WA1": 3, "1C": 4, "2C": 4, "oC": 5}
    arrives = {"FA0": out1, "WA0": out2}
    stage_of = {p + str(n): p + ("A%d" % n if n < 2 else "C") for p in "oFW12" for n in range(3)}
    t_bank = [tok() for b in range(8)]
    tiles = ("o0", "o1", "o2", "F0", "F1", "W0", "W1", "12", "22")
    t_ev = {k: (tok(), tok()) for k in tiles}
    t_q = {k: tok() for k in tiles[2:]}

    def emptied(q, k, halves=(0, 1)):
        for h in halves:
            wait_for(q, t_ev[k][h], 2)

    def product(q, s, i, b, st, mq, ms, m0, start, stop):
        k, n = 512 * i + 128 * b, max(128, width[st[0]])
        if before[st] is not None:
            emptied("PE", before[st], (b // 2,))
        ins = PE.matmul_mx(bank(banks[st] + b, n), q[:, k:k + 128], s[:, k:k + 128], mq[:, m0:m0 + n],
                           ms[:, m0:m0 + n], start, stop)
        if stop:
            done(ins, t_bank[banks[st] + b])

    def layer(st):
        key, p = st[:2] if st[1] == "C" else st, st[0]
        if st in arrives:
            PE.wait_ge(*arrives[st])
        if st[1] == "A":
            for b in range(4):
                product(T.aq, T.asc, int(st[2]), b, st, T.lq, T.lp, x_col[p], True, True)
            return
        steps = [(int(st[2]), b) for b in range(4)] if len(st) == 3 else [(i, b) for b in range(4) for i in range(2)]
        for i, b in steps:
            if p != "o":
                wait_for("PE", t_q[("W" if p == "2" else "F") + str(i)], 1)
            wait("PE", t_c if 512 * i + 128 * b < EARLY else t_c2)
            product(T.cq, T.csc, i, b, key, T.hq, T.hp, h_col[p] + HW * i, i == 0, i == 1)

    def evict(q, k, bs):
        st, p, n = stage_of[k], k[0], int(k[1])
        w = width[p]
        for b in bs:
            wait_for(q, t_bank[banks[st] + b], uses[st])
            src = bank(banks[st] + b, w)
            if n < 2:
                c = h_col[p] + HW * n
                dst = T.hb[:, 4 * c + b:4 * (c + w):4]
                ins = (V.tensor_scalar(dst, src, 0.0, 0.0625, OP.max, OP.mult) if q == "V" else
                       S.activation(dst, src, ACT.Relu, scale=0.0625))
            else:
                dst = T.zb[:, 4 * z_col[p] + b:4 * (z_col[p] + w):4]
                ins = (V.tensor_scalar(dst, src, 0.0625, None, OP.mult) if q == "V" else
                       S.activation(dst, src, ACT.Identity, scale=0.0625))
            done(ins, t_ev[k][b // 2])

    def quantise(k):
        p, n = k[0], int(k[1])
        if p == "F":
            emptied("V", "o%d" % n)
        emptied("V", k)
        if n < 2:
            pack(T.hq, T.hp, h_col[p] + HW * n, T.hb, h_col[p] + HW * n, HW, t_q[k])
        elif p == "o":
            pack(T.zl, T.zlp, 0, T.zb, z_col[p] - PAD, 128, t_q[k])
        elif p == "1":
            pack(T.zq, T.zp, 0, T.zb, 0, 128, t_q[k])
        else:
            pack(T.zq, T.zp, 128, T.zb, z_col[p], HW, t_q[k])

    t_qe = tok()

    def follow(q, steps):
        for w in steps.split():
            if w[0] == "e":
                evict(q, w[1:3], [int(b) for b in w[4:]])
            elif w[0] == "q":
                quantise(w[1:3])
            else:
                wait("V", t_e)
                for b in [int(b) for b in w[1:]]:
                    e0 = EW * (b % 2) + 2 - b // 2 * 2
                    done(V.quantize_mx(T.eq[:, 128 * b:128 * b + 128], T.esc[:, 128 * b:128 * b + 128],
                                       T.ebf[:, e0:e0 + 512]), t_qe)

    wait("V", t_d)
    done(V.tensor_tensor_scan(T.d2[:], T.d0[:, 0:4 * NL], T.d1[:, 0:4 * NL], 0.0, OP.add, OP.min), tv)
    first, rest = ON_VECTOR.split(" ", 1)
    follow("V", first)
    wait("V", tv)
    t_h = done(V.tensor_copy(T.hoff[:], T.d2[:, 3:4 * NL:4]))

    wait("PE", t_a, t_q3)
    for st in ON_TENSOR.split():
        layer(st)
    follow("V", rest)
    follow("S", ON_SCALAR)

    wait("G", t_q["12"])
    home1 = wave([(far1, far_eng, PAD, F1)], T.zq, T.zp, T.zl, T.zlp, T.sem.home1)
    wait("G", t_q["22"])
    home2 = wave([(far2, far_eng, 128, F2), (near, near_eng, 128 + C, NR)], T.zq, T.zp, T.zl, T.zlp, T.sem.home2)

    wait("S", t_h, t_tab, t_xw)
    t_olr = done(S.activation(T.olr[:], T.tab[:].indirect(T.hoff[:]), ACT.Copy))

    def decode(b0, s, ts):
        m0 = PAD + C * s
        for b in UNPACK:
            t = done(PE.matmul_mx(bank(b0 + b, HW), T.eq[:, 128 * b:128 * b + 128], T.esc[:, 128 * b:128 * b + 128],
                                  T.zl[:, m0:m0 + HW], T.zlp[:, m0:m0 + HW], True, True), t_bank[b0 + b])
            dst, src = T.dw[:, DW * b + C * s:DW * b + C * s + HW], bank(b0 + b, HW)
            if b == RAW:
                wait("S", t)
                done(S.activation(dst, src, ACT.Copy), ts[b])
            else:
                wait("V", t)
                done(V.tensor_tensor(dst, src, T.xb[:, 4 * m0 + b:4 * (m0 + HW):4], OP.add), ts[b])

    t_first = tok()
    t_dn = [tok() for b in range(4)]
    wait("V", t_h, t_xw, t_v)
    t_qv = done(V.quantize_mx(T.vq[:], T.vsc[:], T.vs[:]))
    wait("PE", t_qe)
    emptied("PE", "22")
    PE.wait_ge(*home1)
    wait("PE", t_q["o2"])
    decode(0, 0, [t_first] * 4)
    wait("SY", t_olr, t_first)
    t_out = done(SY.dma_start(T.ol[:], T.olr[0:128:16, :]), k=16)
    emptied("PE", "o2")
    PE.wait_ge(*home2)
    decode(4, 2, t_dn)
    wait("V", t_first)
    wait("S", t_first)
    wait("PE", t_first, t_qv)

    ty = [tok(), tok()]

    def pick_y(q, n, b, c0, c1):
        dst = T.yb[:, 64 * c0 + b:64 * c1:4]
        src = T.dw[:, DW * b:DW * (b + 1)].indirect(T.hoff[:, c0:c1])
        wait(q, t_dn[b])
        if b == RAW:
            done(V.tensor_tensor(dst, src, T.xs[:, 64 * c0 + b:64 * c1:4], OP.add), ty[n])
        else:
            gather(q, dst, src, ty[n])

    mid = HW // 16
    for share in ((0, 1, 0, mid), (0, 2, 0, mid), (1, 1, mid, NL), (1, 2, mid, NL), (1, 3, mid + 2, NL)):
        pick_y("S", *share)
    on_vector = (((0, RAW, 0, mid), (0, 3, 0, mid), (1, RAW, mid, NL)), ((1, 3, mid, mid + 2),))
    tq, tm = [None, None], [None, None]
    for n, (j0, j1) in enumerate(runs):
        for share in on_vector[n]:
            pick_y("V", *share)
        wait("V", ty[n])
        tq[n] = pack(T.yq, T.ysc, j0, T.yb, j0, j1 - j0)
        wait("PE", tq[n])
        tm[n] = done(PE.matmul_mx(bank(n, j1 - j0), T.vq[:], T.vsc[:], T.yq[:, j0:j1], T.ysc[:, j0:j1],
                                  True, True), t_bank[n])
        wait("SY", tq[n])
        done(SY.dma_start(T.oc[:, 4 * j0:4 * j1], b8(T.yq[:, j0:j1])), t_out, 16)
    wait("S", tm[0])
    te0 = done(S.activation(T.yo[:, 0:HW], bank(0, HW), ACT.Copy))
    wait("S", te0)
    done(S.dma_start(T.y[:, 0:HW], T.yo[:, 0:HW]), t_out, 16)
    wait("V", tm[1])
    te1 = done(V.tensor_copy(T.yo[:, HW:TC], bank(1, TC - HW)))
    wait("S", *tq)
    for k in range(4):
        q = SY if k < 1 else S
        done(q.dma_start(T.osc[4 * k:4 * k + 4, :], T.ysc[32 * k:32 * k + 4, :]), t_out, 16)
    wait("SY", te1)
    done(SY.dma_start(T.y[:, HW:TC], T.yo[:, HW:TC]), t_out, 16)

    g.wait_ge(T.sem.sent, sent[0])
    for t in toks:
        if t is not t_out and max(list(t["w"].values()) + [0]) < t["n"]:
            wait("G", t)
    wait("SY", t_out)
